import numpy as np
import ml_dtypes


def mxq(x, axis, fmt="e4m3"):
    dtype, down = {"e4m3": (ml_dtypes.float8_e4m3fn, 7), "e5m2": (ml_dtypes.float8_e5m2, 14)}[fmt]
    v = np.moveaxis(np.asarray(x, np.float32).astype(ml_dtypes.bfloat16).astype(np.float64), axis, -1)
    blocks = v.reshape(v.shape[:-1] + (-1, 32))
    amax = np.abs(blocks).max(-1, keepdims=True)
    byte = np.maximum(np.where(amax > 0, np.frexp(amax)[1] - 1 + 127, 0) - down, 1)
    scale = np.exp2(byte - 127.0)
    codes = (blocks / scale).astype(np.float32).astype(dtype).astype(np.float64)
    return np.moveaxis((codes * scale).reshape(v.shape), -1, axis)


WIDE = False


def mx_kscale(k):
    if not WIDE:
        return np.ones(k)
    levels = np.array([10, -10, 5, -5, 0])
    if k % 512:
        return np.exp2(np.random.permutation(np.resize(levels, k // 32))).repeat(32)
    a = np.empty((k // 512, 16))
    for p in range(k // 512):
        a[p, :8] = np.random.permutation(np.resize(levels, 8))
        for g in range(8):
            far = levels[np.abs(levels - a[p, g]) >= 10]
            a[p, g + 8] = far[np.random.randint(len(far))]
    return np.exp2(a.ravel()).repeat(32)


def f64(x):
    return np.asarray(x).astype(np.float64)


def striped(idx):
    return np.tile(idx.reshape(-1, 16).T, (8, 1)).astype(np.uint16)


def unstriped(offs):
    return offs[:16].T.reshape(-1).astype(np.int64)


E2M1 = np.array([0.0, 0.5, 1.0, 1.5, 2.0, 3.0, 4.0, 6.0, -0.0, -0.5, -1.0, -1.5, -2.0, -3.0, -4.0, -6.0])


def pack_weight(w, fmt):
    k, n = w.shape
    w = f64(np.asarray(w, np.float32).astype(ml_dtypes.bfloat16)).reshape(k // 32, 32, n)
    amax = np.abs(w).max(1)
    if fmt == "e4m3":
        byte = np.frexp(amax)[1] - 1 + 127 - 7
    else:
        mant, ex = np.frexp(amax / 6.0)
        byte = np.where(mant > 0.5, ex, ex - 1) + 127
    byte = np.clip(np.where(amax > 0, byte, 1), 1, 254)
    scaled = (w * np.exp2(127.0 - byte)[:, None, :]).reshape(k, n).astype(np.float32)
    by_word = np.ascontiguousarray(scaled.reshape(k // 512, 128, 4, n).transpose(0, 1, 3, 2))
    if fmt == "e4m3":
        words = by_word.astype(ml_dtypes.float8_e4m3fn).view(np.uint8)
    else:
        c = by_word.astype(ml_dtypes.float4_e2m1fn).view(np.uint8) & 0xF
        words = (c[..., 0::2] | (c[..., 1::2] << 4)).reshape(k // 512, 128, 2 * n)
    return np.ascontiguousarray(words), np.ascontiguousarray(byte.astype(np.uint8).reshape(k // 512, 16, n))


def unpack_weight(words, scales, fmt):
    g, _, n = scales.shape
    words = np.ascontiguousarray(words).reshape(g, 128, n, -1)
    if fmt == "e4m3":
        vals = words.view(ml_dtypes.float8_e4m3fn).astype(np.float64)
    else:
        nib = np.empty((g, 128, n, 4), np.uint8)
        nib[..., 0::2] = words & 0xF
        nib[..., 1::2] = words >> 4
        vals = E2M1[nib]
    vals = vals * np.repeat(np.exp2(scales.astype(np.float64) - 127.0), 8, axis=1)[..., None]
    return vals.transpose(0, 1, 3, 2).reshape(g * 512, n)


def gelu(v):
    return 0.5 * v * (1.0 + np.tanh(np.sqrt(2.0 / np.pi) * (v + 0.044715 * v**3)))


def striped8(idx):
    return np.concatenate([v.reshape(-1, 16).T for v in idx]).astype(np.uint16)


def unstriped8(offs):
    return np.stack([offs[16 * g:16 * g + 16].T.reshape(-1) for g in range(8)]).astype(np.int64)


def put_heads(h, wgs, idx8, t2):
    r = np.arange(h.shape[0])
    page = np.zeros((h.shape[0], t2))
    page[r[:, None], idx8[r % 512 // 64]] = wgs[r // 4 % 128] * h
    return page


K, T, S, H, T2, N = 1024, 2048, 512, 1024, 1024, 384

def setup_inputs():
    n = np.random.standard_normal
    s = mx_kscale(K)[:, None]
    u = mx_kscale(H)[:, None]
    tab_words, tab_scales = pack_weight(n((K, T)) * s, "e4m3")
    wa = (n((K, H)) / np.sqrt(K) / s).astype(np.float32)
    wb_words, wb_scales = pack_weight(1.5 * n((K, H)) / np.sqrt(K) / s, "e2m1")
    wf_words, wf_scales = pack_weight(n((H, N)) / np.sqrt(H) / u, "e4m3")
    gain = (np.exp(0.3 * n(H)) * u[:, 0]).astype(np.float32)
    shown = (n((H, T2)) * u).astype(np.float32)
    offs = striped(np.random.permutation(T)[:S])
    offs2 = striped8(np.stack([np.random.permutation(T2)[:S] for _ in range(8)]))
    wgs = np.repeat(np.random.uniform(0.5, 2.0, (8, S)), 16, axis=0).astype(np.float32)
    return {"tab_words": tab_words, "tab_scales": tab_scales, "offs": offs,
            "wa": wa, "wb_words": wb_words, "wb_scales": wb_scales, "gain": gain,
            "offs2": offs2, "wgs": wgs, "shown": shown,
            "wf_words": wf_words, "wf_scales": wf_scales}

def reference(tab_words, tab_scales, offs, wa, wb_words, wb_scales, gain, offs2, wgs, shown, wf_words, wf_scales):
    v = unpack_weight(tab_words, tab_scales, "e4m3")[:, unstriped(offs)]
    wb = unpack_weight(wb_words, wb_scales, "e2m1")
    wf = unpack_weight(wf_words, wf_scales, "e4m3")
    a = mxq(f64(wa), 0, "e4m3").T @ v
    b = wb.T @ v
    h = f64(gain)[:, None] * (np.tanh(a) + 1.0 / (1.0 + np.exp(-b)))
    page = put_heads(h, f64(wgs), unstriped8(offs2), T2)
    z = np.abs(page - f64(shown))
    return wf.T @ mxq(z, 0, "e4m3")

@@ -1,0 +1,307 @@
+from contextlib import ExitStack
+
+import concourse.mybir as mybir
+from concourse.masks import make_identity
+
+K, T, S, H, T2, N = 1024, 2048, 512, 1024, 1024, 384
+FLOPS = 2 * (2 * K * H * S + H * N * T2)
+
+F32 = mybir.dt.float32
+BF16 = mybir.dt.bfloat16
+I32 = mybir.dt.int32
+U32 = mybir.dt.uint32
+U16 = mybir.dt.uint16
+U8 = mybir.dt.uint8
+FP8X4 = mybir.dt.float8_e4m3fn_x4
+FP4X4 = mybir.dt.float4_e2m1fn_x4
+ALU = mybir.AluOpType
+ACT = mybir.ActivationFunctionType
+P = 128
+
+
+def tile_list_carousel_tile_freshness_kernel(
+    tc, tab_words, tab_scales, offs, wa, wb_words, wb_scales, gain, offs2, wgs, shown, wf_words, wf_scales, out
+):
+    nc = tc.nc
+    with ExitStack() as ctx:
+        keep = ctx.enter_context(tc.tile_pool(name="keep", bufs=1))
+        ring = ctx.enter_context(tc.tile_pool(name="ring", bufs=1))
+        psum = ctx.enter_context(tc.psum_pool(name="psum", bufs=1))
+
+        def kt(name, shape, dt):
+            return keep.tile(shape, dt, name=name, align_bytes=64)
+
+        offs_t = keep.tile([P, S // 16], U16, name="offs_t")
+        offs2_t = keep.tile([P, S // 16], U16, name="offs2_t")
+        tab_sc = kt("tab_sc", [P, 2, T], U8)
+        wb_sc_raw = kt("wb_sc_raw", [P, 2, H], U8)
+        wf_sc = kt("wf_sc", [P, N], U8)
+        warm = kt("warm", [P, 8], F32)
+        nc.vector.memset(tab_sc[:].rearrange("p a t -> p (a t)").bitcast(I32), 0)
+        nc.vector.memset(wb_sc_raw[:].rearrange("p a t -> p (a t)").bitcast(I32), 0)
+        nc.vector.memset(warm[:], 0.0)
+        nc.scalar.activation(warm[:, 4:5], warm[:, 0:1], ACT.Sigmoid)
+        nc.vector.memset(wf_sc[:].bitcast(I32), 0)
+        pages = [kt(f"page{i}", [P, T2], F32) for i in range(4)]
+        for i in range(4):
+            nc.vector.memset(pages[i][:], 0.0)
+        ident = kt("ident", [P, P], F32)
+        make_identity(nc, ident[:])
+
+        tabw = [kt(f"tabw{a}", [P, T], I32) for a in range(2)]
+        wb_raw = kt("wb_raw", [P, 2, H // 2], I32)
+        wa_raw = {}
+
+        def load_wa(a, b, c0, c1):
+            t = kt(f"wa_raw{a}{b}{c0}", [P, 4, c1 - c0], F32)
+            nc.sync.dma_start(
+                out=t[:],
+                in_=wa[512 * a : 512 * a + 512, 512 * b + c0 : 512 * b + c1].rearrange("(p j) c -> p j c", j=4),
+            )
+            wa_raw[a, b, c0] = t
+
+        nc.sync.dma_start(offs_t[:], offs)
+        nc.sync.dma_start(out=tabw[0][:], in_=tab_words[0].rearrange("p t i -> p (t i)").bitcast(I32))
+        for q in range(4):
+            nc.sync.dma_start(
+                out=tab_sc[32 * q : 32 * q + 4, :, :].bitcast(I32),
+                in_=tab_scales[:, 4 * q : 4 * q + 4, :].rearrange("a r t -> r a t").bitcast(I32),
+            )
+        load_wa(0, 0, 0, 512)
+        nc.sync.dma_start(out=wb_raw[:], in_=wb_words.rearrange("a p c -> p a c").bitcast(I32))
+        for q in range(4):
+            nc.sync.dma_start(
+                out=wb_sc_raw[32 * q : 32 * q + 4, :, :].bitcast(I32),
+                in_=wb_scales[:, 4 * q : 4 * q + 4, :].rearrange("a r t -> r a t").bitcast(I32),
+            )
+        nc.sync.dma_start(out=tabw[1][:], in_=tab_words[1].rearrange("p t i -> p (t i)").bitcast(I32))
+        load_wa(1, 0, 0, 256)
+        load_wa(1, 0, 256, 512)
+        wgs_t = kt("wgs_t", [P, S], F32)
+        gain_t = kt("gain_t", [P, 2, 4], F32)
+        nc.sync.dma_start(out=gain_t[:], in_=gain.rearrange("(b p i) -> p b i", b=2, i=4))
+        nc.sync.dma_start(out=wgs_t[:], in_=wgs)
+        nc.sync.dma_start(offs2_t[:], offs2)
+        load_wa(0, 1, 0, 512)
+        load_wa(1, 1, 0, 512)
+        shown_t = {}
+        for b in range(2):
+            for u in range(2):
+                t = kt(f"shown{b}{u}", [P, 2, T2], F32)
+                nc.sync.dma_start(
+                    out=t[:],
+                    in_=shown[512 * b : 512 * b + 512, :].rearrange("(p i) m -> p i m", i=4)[:, 2 * u : 2 * u + 2, :],
+                )
+                shown_t[b, u] = t
+        wf_w = [kt(f"wf_w{b}", [P, N], I32) for b in range(2)]
+        for b in range(2):
+            nc.sync.dma_start(out=wf_w[b][:], in_=wf_words[b].rearrange("p c i -> p (c i)").bitcast(I32))
+        for q in range(4):
+            nc.sync.dma_start(
+                out=wf_sc[32 * q : 32 * q + 8, :].bitcast(I32),
+                in_=wf_scales[:, 4 * q : 4 * q + 4, :].bitcast(I32),
+            )
+
+        v_w = [kt(f"v_w{a}", [P, S], U32) for a in range(2)]
+        v_s = [kt(f"v_s{a}", [P, S], U8) for a in range(2)]
+        wb_w = [kt(f"wb_w{a}", [P, 2 * H], U8) for a in range(2)]
+        wb_s = [kt(f"wb_s{a}", [P, H], U8) for a in range(2)]
+        wa_w = {}
+        wa_s = {}
+
+        def gather_words(a):
+            nc.vector.tensor_copy(v_w[a][:], tabw[a][:].bitcast(U32).indirect(offs_t[:]))
+
+        def gather_scales(a):
+            nc.vector.tensor_copy(v_s[a][:], tab_sc[:, a, :].indirect(offs_t[:]))
+
+        def permute_wb_words(a):
+            nc.vector.tensor_copy(
+                wb_w[a][:].bitcast(U16).rearrange("p (b t m) -> p b m t", b=2, t=4),
+                wb_raw[:, a, :].bitcast(U16).rearrange("p (b m t) -> p b m t", b=2, t=4),
+            )
+
+        def permute_wb_scales(a):
+            nc.vector.tensor_copy(
+                wb_s[a][:].rearrange("p (b t m) -> p b m t", b=2, t=4),
+                wb_sc_raw[:, a, :].rearrange("p (b m t) -> p b m t", b=2, t=4),
+            )
+
+        def cast_wa(copy, grouped, raw, c0, c1, r0):
+            dst = grouped[:].rearrange("p (t mm mp j) -> p mm j mp t", t=4, mp=2, j=4)[:, c0 // 8 : c1 // 8]
+            src = raw[:, :, c0 - r0 : c1 - r0].rearrange("p j (mm mp t) -> p mm j mp t", mp=2, t=4)
+            copy(dst, src)
+
+        def quant_wa(a, b, grouped, c0, c1):
+            nc.vector.quantize_mx(
+                out=wa_w[a, b][:, c0:c1].bitcast(FP8X4), scales=wa_s[a, b][:, c0:c1], in_=grouped[:, 4 * c0 : 4 * c1]
+            )
+
+        for a in range(2):
+            for b in range(2):
+                wa_w[a, b] = kt(f"wa_w{a}{b}", [P, 512], U32)
+                wa_s[a, b] = kt(f"wa_s{a}{b}", [P, 512], U8)
+
+        g00 = kt("g00", [P, 2048], BF16)
+        g10 = kt("g10", [P, 2048], BF16)
+        gather_words(0)
+        gather_scales(0)
+        gather_scales(1)
+        cast_wa(nc.scalar.copy, g00, wa_raw[0, 0, 0], 0, 512, 0)
+        permute_wb_words(0)
+        permute_wb_scales(0)
+        permute_wb_words(1)
+        permute_wb_scales(1)
+        quant_wa(0, 0, g00, 0, 512)
+        gather_words(1)
+        cast_wa(nc.scalar.copy, g10, wa_raw[1, 0, 0], 0, 256, 0)
+        cast_wa(nc.scalar.copy, g10, wa_raw[1, 0, 256], 256, 336, 256)
+        cast_wa(nc.vector.tensor_copy, g10, wa_raw[1, 0, 256], 336, 512, 256)
+        quant_wa(1, 0, g10, 0, 128)
+        quant_wa(1, 0, g10, 128, 256)
+        quant_wa(1, 0, g10, 256, 512)
+
+        gw = {}
+
+        def make_gw(s):
+            b, i = divmod(s, 4)
+            gw[s] = ring.tile([P, S], F32, name=f"gw{s}", tag="gw", bufs=4, align_bytes=64)
+            nc.scalar.activation(gw[s][:], wgs_t[:], ACT.Copy, scale=gain_t[:, b, i : i + 1])
+
+        def stage1(s, ta, sb):
+            b, i = divmod(s, 4)
+            cols = slice(128 * i, 128 * i + 128)
+            pb = psum.tile([P, S], F32, name="pb", tag="mm", bufs=4)
+            for a in range(2):
+                c0 = 512 * b + 128 * i
+                nc.tensor.matmul_mx(
+                    out=pb[:], lhsT=wb_w[a][:, 2 * c0 : 2 * c0 + 256].bitcast(FP4X4), lhsT_scale=wb_s[a][:, c0 : c0 + 128],
+                    rhs=v_w[a][:].bitcast(FP8X4), rhs_scale=v_s[a][:], start=(a == 0), stop=(a == 1),
+                )
+            pa = psum.tile([P, S], F32, name="pa", tag="mm", bufs=4)
+            for a in range(2):
+                nc.tensor.matmul_mx(
+                    out=pa[:], lhsT=wa_w[a, b][:, cols].bitcast(FP8X4), lhsT_scale=wa_s[a, b][:, cols],
+                    rhs=v_w[a][:].bitcast(FP8X4), rhs_scale=v_s[a][:], start=(a == 0), stop=(a == 1),
+                )
+            nc.scalar.activation(sb, pb[:], ACT.Sigmoid)
+            nc.scalar.activation(ta, pa[:], ACT.Tanh)
+
+        nsum = {}
+
+        def group(slices):
+            n = len(slices)
+            ta = ring.tile([P, n * S], F32, name=f"ta{slices[0]}", tag=f"ta_{n}", bufs=3 - n, align_bytes=64)
+            sb = ring.tile([P, n * S], F32, name=f"sb{slices[0]}", tag=f"sb_{n}", bufs=3 - n, align_bytes=64)
+            for k, s in enumerate(slices):
+                stage1(s, ta[:, k * S : (k + 1) * S], sb[:, k * S : (k + 1) * S])
+                make_gw(s)
+            return ta, sb
+
+        def combine(slices, ta, sb, ns):
+            nc.vector.scalar_tensor_tensor(out=ns[:], in0=ta[:], scalar=-1.0, in1=sb[:], op0=ALU.mult, op1=ALU.subtract)
+            for k, s in enumerate(slices):
+                nsum[s] = ns[:, k * S : (k + 1) * S]
+
+        def scatter(s):
+            nc.vector.tensor_tensor(pages[s % 4][:].indirect(offs2_t[:]), nsum[s], gw[s][:], ALU.mult)
+
+        zt = {}
+
+        def diff_pair(b, u):
+            for q in range(4):
+                bank = psum.tile([P, 2, 2, P], F32, name="d1", tag="d1", bufs=2)
+                steps = [(shown_t[b, u][:, e, :], cc, e) for cc in range(2) for e in range(2)]
+                steps += [(pages[2 * u + e][:], cc, e) for e in range(2) for cc in range(2)]
+                for k, (src, cc, e) in enumerate(steps):
+                    c = 2 * q + cc
+                    nc.tensor.matmul(
+                        bank[:, cc, e, :], lhsT=src[:, 128 * c : 128 * c + 128], rhs=ident[:], is_transpose=True,
+                        start=(k == 0), stop=(k == len(steps) - 1),
+                    )
+                zt[b, u, q] = ring.tile([P, 512], BF16, name=f"zt{b}{u}{q}", tag=f"zt{u}{q}", align_bytes=64)
+                nc.scalar.activation(
+                    zt[b, u, q][:].rearrange("m (cc p e) -> m cc p e", cc=2, e=2),
+                    bank[:].rearrange("m cc e p -> m cc p e"),
+                    ACT.Abs,
+                )
+
+        z_w = [kt(f"z_w{b}", [P, T2], U32) for b in range(2)]
+        z_s = [kt(f"z_s{b}", [P, T2], U8) for b in range(2)]
+
+        def back(b, q, copy):
+            bank = psum.tile([P, 2, 2, P], F32, name="d2", tag="d2", bufs=2)
+            for cc in range(2):
+                for u in range(2):
+                    nc.tensor.transpose(
+                        bank[:, cc, u, :], zt[b, u, q][:].bitcast(F32)[:, 128 * cc : 128 * cc + 128], ident[:]
+                    )
+            zi = ring.tile([P, 1024], BF16, name=f"zi{b}{q}", tag="zi", bufs=4, align_bytes=64)
+            copy(
+                zi[:].bitcast(F32).rearrange("p (cc m u) -> p cc m u", cc=2, u=2),
+                bank[:].rearrange("p cc u m -> p cc m u"),
+            )
+            cols = slice(256 * q, 256 * q + 256)
+            nc.vector.quantize_mx(out=z_w[b][:, cols].bitcast(FP8X4), scales=z_s[b][:, cols], in_=zi[:])
+
+        t0 = group([0])
+        t12 = group([1, 2])
+        t3 = group([3])
+        combine([0], *t0, kt("ns0", [P, S], F32))
+        scatter(0)
+        combine([1, 2], *t12, kt("ns12", [P, 2 * S], F32))
+        scatter(1)
+        scatter(2)
+        held = ring.tile([P, 4096], BF16, name="g1", tag="held", align_bytes=64)
+        for a in range(2):
+            for h in range(2):
+                cast_wa(nc.scalar.copy, held[:, 2048 * a : 2048 * a + 2048], wa_raw[a, 1, 0], 256 * h, 256 * h + 256, 0)
+        for a in range(2):
+            quant_wa(a, 1, held[:, 2048 * a : 2048 * a + 2048], 0, 512)
+        diff_pair(0, 0)
+        ns3 = ring.tile([P, S], F32, name="ns3", tag="held", align_bytes=64)
+        combine([3], *t3, ns3)
+        t4 = group([4])
+        t5 = group([5])
+        scatter(3)
+        t67 = group([6, 7])
+        combine([4], *t4, kt("ns4", [P, S], F32))
+        scatter(4)
+        diff_pair(0, 1)
+        combine([5], *t5, kt("ns5", [P, S], F32))
+        scatter(5)
+        combine([6, 7], *t67, kt("ns67", [P, 2 * S], F32))
+        for q in range(4):
+            back(0, q, nc.scalar.copy)
+        scatter(6)
+        diff_pair(1, 0)
+        scatter(7)
+
+        def final_pass(acc, n, h, b):
+            cols = slice(512 * h, 512 * h + 512)
+            nc.tensor.matmul_mx(
+                out=acc[:], lhsT=wf_w[b][:, 128 * n : 128 * n + 128].bitcast(FP8X4),
+                lhsT_scale=wf_sc[4 * b :, 128 * n : 128 * n + 128],
+                rhs=z_w[b][:, cols].bitcast(FP8X4), rhs_scale=z_s[b][:, cols], start=(b == 0), stop=(b == 1),
+            )
+
+        order = [(n, h) for h in range(2) for n in range(3)]
+        acc = {}
+        for n, h in order[:4]:
+            acc[n, h] = psum.tile([P, 512], F32, name="acc", tag="mm", bufs=4)
+            final_pass(acc[n, h], n, h, 0)
+        diff_pair(1, 1)
+        for h in range(2):
+            back(1, 2 * h, nc.vector.tensor_copy)
+            back(1, 2 * h + 1, nc.vector.tensor_copy)
+            for n in range(3):
+                if (n, h) not in acc:
+                    acc[n, h] = psum.tile([P, 512], F32, name="acc", tag="mm", bufs=4)
+                    final_pass(acc[n, h], n, h, 0)
+                final_pass(acc[n, h], n, h, 1)
+                res = kt(f"res{n}{h}", [P, 512], F32)
+                if n == 1:
+                    nc.vector.tensor_copy(res[:], acc[n, h][:])
+                else:
+                    nc.scalar.copy(res[:], acc[n, h][:])
+                nc.sync.dma_start(out=out[128 * n : 128 * n + 128, 512 * h : 512 * h + 512], in_=res[:])

@@ -37,14 +37,14 @@ def tile_list_carousel_tile_freshness_kernel(
         wb_sc_raw = kt("wb_sc_raw", [P, 2, H], U8)
         wf_sc = kt("wf_sc", [P, N], U8)
         warm = kt("warm", [P, 8], F32)
-        nc.vector.memset(tab_sc[:].rearrange("p a t -> p (a t)").bitcast(I32), 0)
+        nc.gpsimd.memset(tab_sc[:].rearrange("p a t -> p (a t)").bitcast(I32), 0)
         nc.vector.memset(wb_sc_raw[:].rearrange("p a t -> p (a t)").bitcast(I32), 0)
         nc.vector.memset(warm[:], 0.0)
         nc.scalar.activation(warm[:, 4:5], warm[:, 0:1], ACT.Sigmoid)
         nc.vector.memset(wf_sc[:].bitcast(I32), 0)
         pages = [kt(f"page{i}", [P, T2], F32) for i in range(4)]
         for i in range(4):
-            nc.vector.memset(pages[i][:], 0.0)
+            nc.gpsimd.memset(pages[i][:], 0.0)
         ident = kt("ident", [P, P], F32)
         make_identity(nc, ident[:])
 
@@ -60,28 +60,28 @@ def tile_list_carousel_tile_freshness_kernel(
             )
             wa_raw[a, b, c0] = t
 
+        wgs_t = kt("wgs_t", [P, S], F32)
+        gain_t = kt("gain_t", [P, 2, 4], F32)
         nc.sync.dma_start(offs_t[:], offs)
-        nc.sync.dma_start(out=tabw[0][:], in_=tab_words[0].rearrange("p t i -> p (t i)").bitcast(I32))
+        nc.sync.dma_start(out=wb_raw[:], in_=wb_words.rearrange("a p c -> p a c").bitcast(I32))
+        nc.sync.dma_start(offs2_t[:], offs2)
         for q in range(4):
             nc.sync.dma_start(
                 out=tab_sc[32 * q : 32 * q + 4, :, :].bitcast(I32),
                 in_=tab_scales[:, 4 * q : 4 * q + 4, :].rearrange("a r t -> r a t").bitcast(I32),
             )
-        load_wa(0, 0, 0, 512)
-        nc.sync.dma_start(out=wb_raw[:], in_=wb_words.rearrange("a p c -> p a c").bitcast(I32))
+        nc.sync.dma_start(out=tabw[0][:], in_=tab_words[0].rearrange("p t i -> p (t i)").bitcast(I32))
         for q in range(4):
             nc.sync.dma_start(
                 out=wb_sc_raw[32 * q : 32 * q + 4, :, :].bitcast(I32),
                 in_=wb_scales[:, 4 * q : 4 * q + 4, :].rearrange("a r t -> r a t").bitcast(I32),
             )
+        load_wa(0, 0, 0, 512)
         nc.sync.dma_start(out=tabw[1][:], in_=tab_words[1].rearrange("p t i -> p (t i)").bitcast(I32))
         load_wa(1, 0, 0, 256)
         load_wa(1, 0, 256, 512)
-        wgs_t = kt("wgs_t", [P, S], F32)
-        gain_t = kt("gain_t", [P, 2, 4], F32)
-        nc.sync.dma_start(out=gain_t[:], in_=gain.rearrange("(b p i) -> p b i", b=2, i=4))
         nc.sync.dma_start(out=wgs_t[:], in_=wgs)
-        nc.sync.dma_start(offs2_t[:], offs2)
+        nc.sync.dma_start(out=gain_t[:], in_=gain.rearrange("(b p i) -> p b i", b=2, i=4))
         load_wa(0, 1, 0, 512)
         load_wa(1, 1, 0, 512)
         shown_t = {}
@@ -144,58 +144,64 @@ def tile_list_carousel_tile_freshness_kernel(
 
         g00 = kt("g00", [P, 2048], BF16)
         g10 = kt("g10", [P, 2048], BF16)
-        gather_words(0)
+        permute_wb_words(0)
+        permute_wb_words(1)
         gather_scales(0)
         gather_scales(1)
-        cast_wa(nc.scalar.copy, g00, wa_raw[0, 0, 0], 0, 512, 0)
-        permute_wb_words(0)
+        gather_words(0)
         permute_wb_scales(0)
-        permute_wb_words(1)
         permute_wb_scales(1)
+        cast_wa(nc.scalar.copy, g00, wa_raw[0, 0, 0], 0, 256, 0)
+        cast_wa(nc.vector.tensor_copy, g00, wa_raw[0, 0, 0], 256, 512, 0)
         quant_wa(0, 0, g00, 0, 512)
         gather_words(1)
-        cast_wa(nc.scalar.copy, g10, wa_raw[1, 0, 0], 0, 256, 0)
-        cast_wa(nc.scalar.copy, g10, wa_raw[1, 0, 256], 256, 336, 256)
-        cast_wa(nc.vector.tensor_copy, g10, wa_raw[1, 0, 256], 336, 512, 256)
+        cast_wa(nc.vector.tensor_copy, g10, wa_raw[1, 0, 0], 0, 256, 0)
+        cast_wa(nc.scalar.copy, g10, wa_raw[1, 0, 256], 256, 368, 256)
+        cast_wa(nc.vector.tensor_copy, g10, wa_raw[1, 0, 256], 368, 512, 256)
         quant_wa(1, 0, g10, 0, 128)
         quant_wa(1, 0, g10, 128, 256)
         quant_wa(1, 0, g10, 256, 512)
 
         gw = {}
 
-        def make_gw(s):
+        def make_gw(s, dst):
             b, i = divmod(s, 4)
-            gw[s] = ring.tile([P, S], F32, name=f"gw{s}", tag="gw", bufs=4, align_bytes=64)
-            nc.scalar.activation(gw[s][:], wgs_t[:], ACT.Copy, scale=gain_t[:, b, i : i + 1])
+            gw[s] = dst
+            nc.scalar.activation(dst, wgs_t[:], ACT.Copy, scale=gain_t[:, b, i : i + 1])
 
-        def stage1(s, ta, sb):
+        def taste(s, ta):
             b, i = divmod(s, 4)
             cols = slice(128 * i, 128 * i + 128)
-            pb = psum.tile([P, S], F32, name="pb", tag="mm", bufs=4)
-            for a in range(2):
-                c0 = 512 * b + 128 * i
-                nc.tensor.matmul_mx(
-                    out=pb[:], lhsT=wb_w[a][:, 2 * c0 : 2 * c0 + 256].bitcast(FP4X4), lhsT_scale=wb_s[a][:, c0 : c0 + 128],
-                    rhs=v_w[a][:].bitcast(FP8X4), rhs_scale=v_s[a][:], start=(a == 0), stop=(a == 1),
-                )
-            pa = psum.tile([P, S], F32, name="pa", tag="mm", bufs=4)
+            pa = psum.tile([P, S], F32, name="pa", tag="x", bufs=4)
             for a in range(2):
                 nc.tensor.matmul_mx(
                     out=pa[:], lhsT=wa_w[a, b][:, cols].bitcast(FP8X4), lhsT_scale=wa_s[a, b][:, cols],
                     rhs=v_w[a][:].bitcast(FP8X4), rhs_scale=v_s[a][:], start=(a == 0), stop=(a == 1),
                 )
-            nc.scalar.activation(sb, pb[:], ACT.Sigmoid)
             nc.scalar.activation(ta, pa[:], ACT.Tanh)
+
+        def appeal(s, sb, tag, bufs):
+            c0 = 128 * s
+            pb = psum.tile([P, S], F32, name="pb", tag=tag, bufs=bufs)
+            for a in range(2):
+                nc.tensor.matmul_mx(
+                    out=pb[:], lhsT=wb_w[a][:, 2 * c0 : 2 * c0 + 256].bitcast(FP4X4), lhsT_scale=wb_s[a][:, c0 : c0 + 128],
+                    rhs=v_w[a][:].bitcast(FP8X4), rhs_scale=v_s[a][:], start=(a == 0), stop=(a == 1),
+                )
+            nc.scalar.activation(sb, pb[:], ACT.Sigmoid)
 
         nsum = {}
 
-        def group(slices):
+        def rt(name, cols, tag):
+            return ring.tile([P, cols], F32, name=name, tag=tag, align_bytes=64)
+
+        def group(slices, tag):
             n = len(slices)
-            ta = ring.tile([P, n * S], F32, name=f"ta{slices[0]}", tag=f"ta_{n}", bufs=3 - n, align_bytes=64)
-            sb = ring.tile([P, n * S], F32, name=f"sb{slices[0]}", tag=f"sb_{n}", bufs=3 - n, align_bytes=64)
+            ta = rt(f"ta{slices[0]}", n * S, "ta" + tag)
+            sb = rt(f"sb{slices[0]}", n * S, "sb" + tag)
             for k, s in enumerate(slices):
-                stage1(s, ta[:, k * S : (k + 1) * S], sb[:, k * S : (k + 1) * S])
-                make_gw(s)
+                taste(s, ta[:, k * S : (k + 1) * S])
+                appeal(s, sb[:, k * S : (k + 1) * S], "x", 4)
             return ta, sb
 
         def combine(slices, ta, sb, ns):
@@ -204,50 +210,80 @@ def tile_list_carousel_tile_freshness_kernel(
                 nsum[s] = ns[:, k * S : (k + 1) * S]
 
         def scatter(s):
-            nc.vector.tensor_tensor(pages[s % 4][:].indirect(offs2_t[:]), nsum[s], gw[s][:], ALU.mult)
+            nc.vector.tensor_tensor(pages[s % 4][:].indirect(offs2_t[:]), nsum[s], gw[s], ALU.mult)
 
         zt = {}
 
-        def diff_pair(b, u):
-            for q in range(4):
-                bank = psum.tile([P, 2, 2, P], F32, name="d1", tag="d1", bufs=2)
-                steps = [(shown_t[b, u][:, e, :], cc, e) for cc in range(2) for e in range(2)]
-                steps += [(pages[2 * u + e][:], cc, e) for e in range(2) for cc in range(2)]
-                for k, (src, cc, e) in enumerate(steps):
-                    c = 2 * q + cc
-                    nc.tensor.matmul(
-                        bank[:, cc, e, :], lhsT=src[:, 128 * c : 128 * c + 128], rhs=ident[:], is_transpose=True,
-                        start=(k == 0), stop=(k == len(steps) - 1),
-                    )
-                zt[b, u, q] = ring.tile([P, 512], BF16, name=f"zt{b}{u}{q}", tag=f"zt{u}{q}", align_bytes=64)
+        def add_transpose(dst, src, c, start, stop):
+            nc.tensor.matmul(dst, lhsT=src[:, 128 * c : 128 * c + 128], rhs=ident[:], is_transpose=True, start=start, stop=stop)
+
+        def diff_pair(b, u, order):
+            for h in range(2):
+                zt[u, h] = ring.tile([P, 1024], BF16, name=f"zt{b}{u}{h}", tag=f"zt{u}{h}", align_bytes=64)
+            bank = {}
+            for q in order:
+                bank[q] = psum.tile([P, 2, 2, P], F32, name="d1", tag="x", bufs=4)
+                for cc in range(2):
+                    for e in range(2):
+                        add_transpose(bank[q][:, cc, e, :], shown_t[b, u][:, e, :], 2 * q + cc, cc + e == 0, False)
+                for cc in range(2):
+                    add_transpose(bank[q][:, cc, 0, :], pages[2 * u][:], 2 * q + cc, False, False)
+            for q in order:
+                for cc in range(2):
+                    add_transpose(bank[q][:, cc, 1, :], pages[2 * u + 1][:], 2 * q + cc, False, cc == 1)
                 nc.scalar.activation(
-                    zt[b, u, q][:].rearrange("m (cc p e) -> m cc p e", cc=2, e=2),
-                    bank[:].rearrange("m cc e p -> m cc p e"),
+                    zt[u, q // 2][:, 512 * (q % 2) : 512 * (q % 2) + 512].rearrange("m (cc p e) -> m cc p e", cc=2, e=2),
+                    bank[q][:].rearrange("m cc e p -> m cc p e"),
                     ACT.Abs,
                 )
 
-        z_w = [kt(f"z_w{b}", [P, T2], U32) for b in range(2)]
-        z_s = [kt(f"z_s{b}", [P, T2], U8) for b in range(2)]
+        z_w = {}
+        z_s = {(b, h): kt(f"z_s{b}{h}", [P, 512], U8) for b in range(2) for h in range(2)}
+        for b, h in ((0, 0), (0, 1), (1, 0), (1, 1)):
+            z_w[b, h] = kt(f"z_w{b}{h}", [P, 512], U32)
 
-        def back(b, q, copy):
-            bank = psum.tile([P, 2, 2, P], F32, name="d2", tag="d2", bufs=2)
-            for cc in range(2):
-                for u in range(2):
+        def back(q, zi):
+            bank = psum.tile([P, 2, 2, P], F32, name="d2", tag="x", bufs=4)
+            for u in range(2):
+                for cc in range(2):
+                    c = 2 * (q % 2) + cc
                     nc.tensor.transpose(
-                        bank[:, cc, u, :], zt[b, u, q][:].bitcast(F32)[:, 128 * cc : 128 * cc + 128], ident[:]
+                        bank[:, cc, u, :], zt[u, q // 2][:].bitcast(F32)[:, 128 * c : 128 * c + 128], ident[:]
                     )
-            zi = ring.tile([P, 1024], BF16, name=f"zi{b}{q}", tag="zi", bufs=4, align_bytes=64)
-            copy(
-                zi[:].bitcast(F32).rearrange("p (cc m u) -> p cc m u", cc=2, u=2),
+            nc.scalar.copy(
+                zi.bitcast(F32).rearrange("p (cc m u) -> p cc m u", cc=2, u=2),
                 bank[:].rearrange("p cc u m -> p cc m u"),
             )
-            cols = slice(256 * q, 256 * q + 256)
-            nc.vector.quantize_mx(out=z_w[b][:, cols].bitcast(FP8X4), scales=z_s[b][:, cols], in_=zi[:])
 
-        t0 = group([0])
-        t12 = group([1, 2])
-        t3 = group([3])
-        combine([0], *t0, kt("ns0", [P, S], F32))
+        def back_half(h, dst):
+            bank = psum.tile([P, 4, P], F32, name="d3", tag="y", bufs=2)
+            for cc in range(4):
+                nc.tensor.transpose(bank[:, cc, :], zt[0, h][:].bitcast(F32)[:, 128 * cc : 128 * cc + 128], ident[:])
+            for k in (1, 0):
+                nc.scalar.copy(
+                    dst[k][:].bitcast(F32).rearrange("p (mm u x) -> p mm u x", u=2, x=4)[:, :, 0, :],
+                    bank[:, 2 * k : 2 * k + 2, :].rearrange("p cc (mm x) -> p (cc mm) x", x=4),
+                )
+
+        def quant_z(b, m0, m1, zi):
+            h, c0, c1 = m0 // 512, m0 % 512, (m1 - 1) % 512 + 1
+            nc.vector.quantize_mx(out=z_w[b, h][:, c0:c1].bitcast(FP8X4), scales=z_s[b, h][:, c0:c1], in_=zi)
+
+        t0 = rt("ta0", S, "r0"), rt("sb0", S, "r1")
+        t12 = rt("ta1", 2 * S, "taB"), rt("sb1", 2 * S, "sbB")
+        t3 = rt("ta3", S, "taA"), rt("sb3", S, "sbA")
+        appeal(0, t0[1][:], "y", 2)
+        make_gw(0, kt("gw0", [P, S], F32)[:])
+        taste(0, t0[0][:])
+        taste(1, t12[0][:, 0:S])
+        taste(2, t12[0][:, S : 2 * S])
+        taste(3, t3[0][:])
+        appeal(1, t12[1][:, 0:S], "x", 4)
+        appeal(2, t12[1][:, S : 2 * S], "x", 4)
+        appeal(3, t3[1][:], "x", 4)
+        combine([0], *t0, rt("ns0", S, "r2"))
+        make_gw(1, rt("gw1", S, "r0")[:])
+        make_gw(2, rt("gw2", S, "r1")[:])
         scatter(0)
         combine([1, 2], *t12, kt("ns12", [P, 2 * S], F32))
         scatter(1)
@@ -258,50 +294,88 @@ def tile_list_carousel_tile_freshness_kernel(
                 cast_wa(nc.scalar.copy, held[:, 2048 * a : 2048 * a + 2048], wa_raw[a, 1, 0], 256 * h, 256 * h + 256, 0)
         for a in range(2):
             quant_wa(a, 1, held[:, 2048 * a : 2048 * a + 2048], 0, 512)
-        diff_pair(0, 0)
+        gw_late = rt("gw_late", 5 * S, "r2")
+        for s in range(3, 8):
+            make_gw(s, gw_late[:, (s - 3) * S : (s - 2) * S])
+        diff_pair(0, 0, range(4))
         ns3 = ring.tile([P, S], F32, name="ns3", tag="held", align_bytes=64)
         combine([3], *t3, ns3)
-        t4 = group([4])
-        t5 = group([5])
+        t4 = group([4], "C")
         scatter(3)
-        t67 = group([6, 7])
+        t56 = group([5, 6], "B")
+        t7 = group([7], "A")
         combine([4], *t4, kt("ns4", [P, S], F32))
         scatter(4)
-        diff_pair(0, 1)
-        combine([5], *t5, kt("ns5", [P, S], F32))
+        diff_pair(0, 1, range(4))
+        combine([5, 6], *t56, kt("ns56", [P, 2 * S], F32))
         scatter(5)
-        combine([6, 7], *t67, kt("ns67", [P, 2 * S], F32))
+        zi0 = ring.tile([P, 4096], BF16, name="zi0", tag="held", align_bytes=64)
         for q in range(4):
-            back(0, q, nc.scalar.copy)
+            back(q, zi0[:, 1024 * q : 1024 * q + 1024])
         scatter(6)
-        diff_pair(1, 0)
+        for h in range(2):
+            quant_z(0, 512 * h, 512 * h + 512, zi0[:, 2048 * h : 2048 * h + 2048])
+        last = ring.tile([P, 2 * T2], F32, name="last", tag="held", align_bytes=64)
+        d = last[:].rearrange("p (e m) -> p e m", e=2)
+        ns7 = d[:, 1, 0:S]
+        combine([7], *t7, ns7)
+        nc.vector.tensor_tensor(d[:, 0, :], pages[2][:], shown_t[1, 1][:, 0, :], ALU.add)
+        diff_pair(1, 0, (2, 3, 0, 1))
+        zi1 = [kt(f"zi1{q}", [P, 1024], BF16) for q in range(4)]
+        zp = [kt(f"zp{q}", [P, 1024], BF16) for q in range(4)]
+        for h in (1, 0):
+            back_half(h, zp[2 * h : 2 * h + 2])
         scatter(7)
 
-        def final_pass(acc, n, h, b):
-            cols = slice(512 * h, 512 * h + 512)
+        def final_pass(dst, n, m0, m1, b, start, stop):
             nc.tensor.matmul_mx(
-                out=acc[:], lhsT=wf_w[b][:, 128 * n : 128 * n + 128].bitcast(FP8X4),
+                out=dst, lhsT=wf_w[b][:, 128 * n : 128 * n + 128].bitcast(FP8X4),
                 lhsT_scale=wf_sc[4 * b :, 128 * n : 128 * n + 128],
-                rhs=z_w[b][:, cols].bitcast(FP8X4), rhs_scale=z_s[b][:, cols], start=(b == 0), stop=(b == 1),
+                rhs=z_w[b, m0 // 512][:, m0 % 512 : (m1 - 1) % 512 + 1].bitcast(FP8X4),
+                rhs_scale=z_s[b, m0 // 512][:, m0 % 512 : (m1 - 1) % 512 + 1], start=start, stop=stop,
             )
 
-        order = [(n, h) for h in range(2) for n in range(3)]
-        acc = {}
-        for n, h in order[:4]:
-            acc[n, h] = psum.tile([P, 512], F32, name="acc", tag="mm", bufs=4)
-            final_pass(acc[n, h], n, h, 0)
-        diff_pair(1, 1)
+        acc_a = []
+        for q in range(4):
+            acc_a.append(psum.tile([P, 2, 256], F32, name="acca", tag="x", bufs=4))
+            for n in range(2):
+                final_pass(acc_a[q][:, n, :], n, 256 * q, 256 * q + 256, 0, n == 0, False)
+        acc_b = []
         for h in range(2):
-            back(1, 2 * h, nc.vector.tensor_copy)
-            back(1, 2 * h + 1, nc.vector.tensor_copy)
-            for n in range(3):
-                if (n, h) not in acc:
-                    acc[n, h] = psum.tile([P, 512], F32, name="acc", tag="mm", bufs=4)
-                    final_pass(acc[n, h], n, h, 0)
-                final_pass(acc[n, h], n, h, 1)
-                res = kt(f"res{n}{h}", [P, 512], F32)
-                if n == 1:
-                    nc.vector.tensor_copy(res[:], acc[n, h][:])
-                else:
-                    nc.scalar.copy(res[:], acc[n, h][:])
-                nc.sync.dma_start(out=out[128 * n : 128 * n + 128, 512 * h : 512 * h + 512], in_=res[:])
+            acc_b.append(psum.tile([P, 512], F32, name="accb", tag="y", bufs=2))
+            final_pass(acc_b[h][:], 2, 512 * h, 512 * h + 512, 0, True, False)
+        for q in range(4):
+            cols = slice(256 * q, 256 * q + 256)
+            nc.vector.tensor_tensor(d[:, 1, cols], pages[3][:, cols], shown_t[1, 1][:, 1, cols], ALU.add)
+            nc.scalar.activation(
+                zp[q][:].rearrange("p (mm u x e) -> p mm u x e", u=2, x=4, e=2)[:, :, 1, :, :],
+                d[:, :, cols].rearrange("p e (mm x) -> p mm x e", x=4),
+                ACT.Abs,
+            )
+
+        def store_a(q, copy):
+            res = ring.tile([P, 2, 256], F32, name=f"resa{q}", tag=f"zt{q // 2}{q % 2}", align_bytes=64)
+            copy(res[:], acc_a[q][:])
+            nc.sync.dma_start(out=out[0:256, 256 * q : 256 * q + 256].rearrange("(n p) m -> p n m", n=2), in_=res[:])
+
+        def store_b(h, copy):
+            res = kt(f"resb{h}", [P, 512], F32)
+            copy(res[:], acc_b[h][:])
+            nc.sync.dma_start(out=out[256:384, 512 * h : 512 * h + 512], in_=res[:])
+
+        for q in range(4):
+            nc.vector.tensor_copy(
+                zi1[q][:].bitcast(F32).rearrange("p (mm x u) -> p mm x u", x=4, u=2),
+                zp[q][:].bitcast(F32).rearrange("p (mm u x) -> p mm x u", x=4, u=2),
+            )
+            quant_z(1, 256 * q, 256 * q + 256, zi1[q][:])
+            h = q // 2
+            for n in range(2):
+                final_pass(acc_a[q][:, n, :], n, 256 * q, 256 * q + 256, 1, False, n == 1)
+            final_pass(acc_b[h][:, 256 * (q % 2) : 256 * (q % 2) + 256], 2, 256 * q, 256 * q + 256, 1, False, q % 2 == 1)
+        store_a(0, nc.scalar.copy)
+        store_a(1, nc.scalar.copy)
+        store_b(0, nc.scalar.copy)
+        store_a(2, nc.vector.tensor_copy)
+        store_a(3, nc.vector.tensor_copy)
+        store_b(1, nc.scalar.copy)

@@ -42,9 +42,13 @@ def tile_list_carousel_tile_freshness_kernel(
         nc.vector.memset(warm[:], 0.0)
         nc.scalar.activation(warm[:, 4:5], warm[:, 0:1], ACT.Sigmoid)
         nc.vector.memset(wf_sc[:].bitcast(I32), 0)
-        pages = [kt(f"page{i}", [P, T2], F32) for i in range(4)]
-        for i in range(4):
+        pages = {}
+
+        def new_page(i, tag):
+            pages[i] = ring.tile([P, T2], F32, name=f"page{i}", tag=tag, align_bytes=64)
             nc.gpsimd.memset(pages[i][:], 0.0)
+
+        new_page(0, "page0")
         ident = kt("ident", [P, P], F32)
         make_identity(nc, ident[:])
 
@@ -67,14 +71,14 @@ def tile_list_carousel_tile_freshness_kernel(
         nc.sync.dma_start(offs2_t[:], offs2)
         for q in range(4):
             nc.sync.dma_start(
-                out=tab_sc[32 * q : 32 * q + 4, :, :].bitcast(I32),
-                in_=tab_scales[:, 4 * q : 4 * q + 4, :].rearrange("a r t -> r a t").bitcast(I32),
+                out=tab_sc[q:P:32, :, :].bitcast(I32),
+                in_=tab_scales[:, q:16:4, :].rearrange("a r t -> r a t").bitcast(I32),
             )
         nc.sync.dma_start(out=tabw[0][:], in_=tab_words[0].rearrange("p t i -> p (t i)").bitcast(I32))
         for q in range(4):
             nc.sync.dma_start(
-                out=wb_sc_raw[32 * q : 32 * q + 4, :, :].bitcast(I32),
-                in_=wb_scales[:, 4 * q : 4 * q + 4, :].rearrange("a r t -> r a t").bitcast(I32),
+                out=wb_sc_raw[q:P:32, :, :].bitcast(I32),
+                in_=wb_scales[:, q:16:4, :].rearrange("a r t -> r a t").bitcast(I32),
             )
         load_wa(0, 0, 0, 512)
         nc.sync.dma_start(out=tabw[1][:], in_=tab_words[1].rearrange("p t i -> p (t i)").bitcast(I32))
@@ -143,7 +147,7 @@ def tile_list_carousel_tile_freshness_kernel(
                 wa_s[a, b] = kt(f"wa_s{a}{b}", [P, 512], U8)
 
         g00 = kt("g00", [P, 2048], BF16)
-        g10 = kt("g10", [P, 2048], BF16)
+        g10 = ring.tile([P, 2048], BF16, name="g10", tag="r3", align_bytes=64)
         permute_wb_words(0)
         permute_wb_words(1)
         gather_scales(0)
@@ -273,7 +277,7 @@ def tile_list_carousel_tile_freshness_kernel(
         t12 = rt("ta1", 2 * S, "taB"), rt("sb1", 2 * S, "sbB")
         t3 = rt("ta3", S, "taA"), rt("sb3", S, "sbA")
         appeal(0, t0[1][:], "y", 2)
-        make_gw(0, kt("gw0", [P, S], F32)[:])
+        make_gw(0, rt("gw0", S, "r4")[:])
         taste(0, t0[0][:])
         taste(1, t12[0][:, 0:S])
         taste(2, t12[0][:, S : 2 * S])
@@ -284,9 +288,12 @@ def tile_list_carousel_tile_freshness_kernel(
         combine([0], *t0, rt("ns0", S, "r2"))
         make_gw(1, rt("gw1", S, "r0")[:])
         make_gw(2, rt("gw2", S, "r1")[:])
+        new_page(1, "r3")
         scatter(0)
+        new_page(2, "r4")
         combine([1, 2], *t12, kt("ns12", [P, 2 * S], F32))
         scatter(1)
+        new_page(3, "r0")
         scatter(2)
         held = ring.tile([P, 4096], BF16, name="g1", tag="held", align_bytes=64)
         for a in range(2):

@@ -53,53 +53,65 @@ def tile_list_carousel_tile_freshness_kernel(
         make_identity(nc, ident[:])
 
         tabw = [kt(f"tabw{a}", [P, T], I32) for a in range(2)]
-        wb_raw = kt("wb_raw", [P, 2, H // 2], I32)
+        wb_raw = [
+            ring.tile([P, 2, H // 4], I32, name=f"wb_raw{b}", tag=f"wb_raw{b}", align_bytes=64) for b in range(2)
+        ]
         wa_raw = {}
 
         def load_wa(a, b, c0, c1):
-            t = kt(f"wa_raw{a}{b}{c0}", [P, 4, c1 - c0], F32)
+            t = ring.tile([P, 4, c1 - c0], F32, name=f"wa_raw{a}{b}{c0}", tag=f"wa_raw{a}{b}{c0}", align_bytes=64)
             nc.sync.dma_start(
                 out=t[:],
                 in_=wa[512 * a : 512 * a + 512, 512 * b + c0 : 512 * b + c1].rearrange("(p j) c -> p j c", j=4),
             )
             wa_raw[a, b, c0] = t
 
+        def load_wb(b):
+            nc.sync.dma_start(
+                out=wb_raw[b][:], in_=wb_words[:, :, H * b : H * b + H].rearrange("a p c -> p a c").bitcast(I32)
+            )
+
         wgs_t = kt("wgs_t", [P, S], F32)
         gain_t = kt("gain_t", [P, 2, 4], F32)
         nc.sync.dma_start(offs_t[:], offs)
-        nc.sync.dma_start(out=wb_raw[:], in_=wb_words.rearrange("a p c -> p a c").bitcast(I32))
+        nc.sync.dma_start(out=tabw[0][:], in_=tab_words[0].rearrange("p t i -> p (t i)").bitcast(I32))
         nc.sync.dma_start(offs2_t[:], offs2)
         for q in range(4):
             nc.sync.dma_start(
                 out=tab_sc[q:P:32, :, :].bitcast(I32),
                 in_=tab_scales[:, q:16:4, :].rearrange("a r t -> r a t").bitcast(I32),
             )
-        nc.sync.dma_start(out=tabw[0][:], in_=tab_words[0].rearrange("p t i -> p (t i)").bitcast(I32))
+        load_wb(0)
+        load_wa(0, 0, 0, 512)
         for q in range(4):
             nc.sync.dma_start(
                 out=wb_sc_raw[q:P:32, :, :].bitcast(I32),
                 in_=wb_scales[:, q:16:4, :].rearrange("a r t -> r a t").bitcast(I32),
             )
-        load_wa(0, 0, 0, 512)
         nc.sync.dma_start(out=tabw[1][:], in_=tab_words[1].rearrange("p t i -> p (t i)").bitcast(I32))
         load_wa(1, 0, 0, 256)
         load_wa(1, 0, 256, 512)
         nc.sync.dma_start(out=wgs_t[:], in_=wgs)
         nc.sync.dma_start(out=gain_t[:], in_=gain.rearrange("(b p i) -> p b i", b=2, i=4))
+        load_wb(1)
+        shown_t = {}
+
+        def load_shown(b, u):
+            shown_t[b, u] = kt(f"shown{b}{u}", [P, 2, T2], F32)
+            nc.sync.dma_start(
+                out=shown_t[b, u][:],
+                in_=shown[512 * b : 512 * b + 512, :].rearrange("(p i) m -> p i m", i=4)[:, 2 * u : 2 * u + 2, :],
+            )
+
+        load_shown(0, 0)
         load_wa(0, 1, 0, 512)
         load_wa(1, 1, 0, 512)
-        shown_t = {}
-        for b in range(2):
-            for u in range(2):
-                t = kt(f"shown{b}{u}", [P, 2, T2], F32)
-                nc.sync.dma_start(
-                    out=t[:],
-                    in_=shown[512 * b : 512 * b + 512, :].rearrange("(p i) m -> p i m", i=4)[:, 2 * u : 2 * u + 2, :],
-                )
-                shown_t[b, u] = t
         wf_w = [kt(f"wf_w{b}", [P, N], I32) for b in range(2)]
         for b in range(2):
             nc.sync.dma_start(out=wf_w[b][:], in_=wf_words[b].rearrange("p c i -> p (c i)").bitcast(I32))
+        load_shown(1, 0)
+        load_shown(1, 1)
+        load_shown(0, 1)
         for q in range(4):
             nc.sync.dma_start(
                 out=wf_sc[32 * q : 32 * q + 8, :].bitcast(I32),
@@ -108,7 +120,7 @@ def tile_list_carousel_tile_freshness_kernel(
 
         v_w = [kt(f"v_w{a}", [P, S], U32) for a in range(2)]
         v_s = [kt(f"v_s{a}", [P, S], U8) for a in range(2)]
-        wb_w = [kt(f"wb_w{a}", [P, 2 * H], U8) for a in range(2)]
+        wb_w = [kt(f"wb_w{b}", [P, 2, H], U8) for b in range(2)]
         wb_s = [kt(f"wb_s{a}", [P, H], U8) for a in range(2)]
         wa_w = {}
         wa_s = {}
@@ -119,10 +131,10 @@ def tile_list_carousel_tile_freshness_kernel(
         def gather_scales(a):
             nc.vector.tensor_copy(v_s[a][:], tab_sc[:, a, :].indirect(offs_t[:]))
 
-        def permute_wb_words(a):
+        def permute_wb_words(b):
             nc.vector.tensor_copy(
-                wb_w[a][:].bitcast(U16).rearrange("p (b t m) -> p b m t", b=2, t=4),
-                wb_raw[:, a, :].bitcast(U16).rearrange("p (b m t) -> p b m t", b=2, t=4),
+                wb_w[b][:].bitcast(U16).rearrange("p a (t m) -> p a m t", t=4),
+                wb_raw[b][:].bitcast(U16).rearrange("p a (m t) -> p a m t", t=4),
             )
 
         def permute_wb_scales(a):
@@ -141,23 +153,25 @@ def tile_list_carousel_tile_freshness_kernel(
                 out=wa_w[a, b][:, c0:c1].bitcast(FP8X4), scales=wa_s[a, b][:, c0:c1], in_=grouped[:, 4 * c0 : 4 * c1]
             )
 
+        wa_w1 = kt("wa_w1", [P, 1024], U32)
+        wa_s1 = kt("wa_s1", [P, 1024], U8)
         for a in range(2):
-            for b in range(2):
-                wa_w[a, b] = kt(f"wa_w{a}{b}", [P, 512], U32)
-                wa_s[a, b] = kt(f"wa_s{a}{b}", [P, 512], U8)
+            wa_w[a, 0] = kt(f"wa_w{a}0", [P, 512], U32)
+            wa_s[a, 0] = kt(f"wa_s{a}0", [P, 512], U8)
+            wa_w[a, 1] = wa_w1[:, 512 * a : 512 * a + 512]
+            wa_s[a, 1] = wa_s1[:, 512 * a : 512 * a + 512]
 
         g00 = kt("g00", [P, 2048], BF16)
         g10 = ring.tile([P, 2048], BF16, name="g10", tag="r3", align_bytes=64)
-        permute_wb_words(0)
-        permute_wb_words(1)
+        gather_words(0)
         gather_scales(0)
         gather_scales(1)
-        gather_words(0)
-        permute_wb_scales(0)
-        permute_wb_scales(1)
+        permute_wb_words(0)
         cast_wa(nc.scalar.copy, g00, wa_raw[0, 0, 0], 0, 256, 0)
         cast_wa(nc.vector.tensor_copy, g00, wa_raw[0, 0, 0], 256, 512, 0)
         quant_wa(0, 0, g00, 0, 512)
+        permute_wb_scales(0)
+        permute_wb_scales(1)
         gather_words(1)
         cast_wa(nc.vector.tensor_copy, g10, wa_raw[1, 0, 0], 0, 256, 0)
         cast_wa(nc.scalar.copy, g10, wa_raw[1, 0, 256], 256, 368, 256)
@@ -165,6 +179,7 @@ def tile_list_carousel_tile_freshness_kernel(
         quant_wa(1, 0, g10, 0, 128)
         quant_wa(1, 0, g10, 128, 256)
         quant_wa(1, 0, g10, 256, 512)
+        permute_wb_words(1)
 
         gw = {}
 
@@ -189,7 +204,7 @@ def tile_list_carousel_tile_freshness_kernel(
             pb = psum.tile([P, S], F32, name="pb", tag=tag, bufs=bufs)
             for a in range(2):
                 nc.tensor.matmul_mx(
-                    out=pb[:], lhsT=wb_w[a][:, 2 * c0 : 2 * c0 + 256].bitcast(FP4X4), lhsT_scale=wb_s[a][:, c0 : c0 + 128],
+                    out=pb[:], lhsT=wb_w[s // 4][:, a, 256 * (s % 4) : 256 * (s % 4) + 256].bitcast(FP4X4), lhsT_scale=wb_s[a][:, c0 : c0 + 128],
                     rhs=v_w[a][:].bitcast(FP8X4), rhs_scale=v_s[a][:], start=(a == 0), stop=(a == 1),
                 )
             nc.scalar.activation(sb, pb[:], ACT.Sigmoid)
@@ -199,19 +214,15 @@ def tile_list_carousel_tile_freshness_kernel(
         def rt(name, cols, tag):
             return ring.tile([P, cols], F32, name=name, tag=tag, align_bytes=64)
 
-        def group(slices, tag):
-            n = len(slices)
-            ta = rt(f"ta{slices[0]}", n * S, "ta" + tag)
-            sb = rt(f"sb{slices[0]}", n * S, "sb" + tag)
-            for k, s in enumerate(slices):
-                taste(s, ta[:, k * S : (k + 1) * S])
-                appeal(s, sb[:, k * S : (k + 1) * S], "x", 4)
-            return ta, sb
+        acts = {}
 
-        def combine(slices, ta, sb, ns):
-            nc.vector.scalar_tensor_tensor(out=ns[:], in0=ta[:], scalar=-1.0, in1=sb[:], op0=ALU.mult, op1=ALU.subtract)
-            for k, s in enumerate(slices):
-                nsum[s] = ns[:, k * S : (k + 1) * S]
+        def act_tiles(s):
+            acts[s] = rt(f"ta{s}", S, f"ta{s % 4}"), rt(f"sb{s}", S, f"sb{s % 4}")
+
+        def combine(s):
+            nsum[s] = rt(f"ns{s}", S, f"ns{s % 4}")[:]
+            ta, sb = acts[s]
+            nc.vector.scalar_tensor_tensor(out=nsum[s], in0=ta[:], scalar=-1.0, in1=sb[:], op0=ALU.mult, op1=ALU.subtract)
 
         def scatter(s):
             nc.vector.tensor_tensor(pages[s % 4][:].indirect(offs2_t[:]), nsum[s], gw[s], ALU.mult)
@@ -221,18 +232,22 @@ def tile_list_carousel_tile_freshness_kernel(
         def add_transpose(dst, src, c, start, stop):
             nc.tensor.matmul(dst, lhsT=src[:, 128 * c : 128 * c + 128], rhs=ident[:], is_transpose=True, start=start, stop=stop)
 
-        def diff_pair(b, u, order):
-            for h in range(2):
-                zt[u, h] = ring.tile([P, 1024], BF16, name=f"zt{b}{u}{h}", tag=f"zt{u}{h}", align_bytes=64)
+        def diff_open(b, u, order, tag):
             bank = {}
             for q in order:
-                bank[q] = psum.tile([P, 2, 2, P], F32, name="d1", tag="x", bufs=4)
+                bank[q] = psum.tile([P, 2, 2, P], F32, name="d1", tag=tag, bufs=4)
                 for cc in range(2):
                     for e in range(2):
                         add_transpose(bank[q][:, cc, e, :], shown_t[b, u][:, e, :], 2 * q + cc, cc + e == 0, False)
+            for q in order:
                 for cc in range(2):
                     add_transpose(bank[q][:, cc, 0, :], pages[2 * u][:], 2 * q + cc, False, False)
-            for q in order:
+            return bank
+
+        def diff_close(b, u, bank):
+            for h in range(2):
+                zt[u, h] = ring.tile([P, 1024], BF16, name=f"zt{b}{u}{h}", tag=f"zt{u}{h}", align_bytes=64)
+            for q in bank:
                 for cc in range(2):
                     add_transpose(bank[q][:, cc, 1, :], pages[2 * u + 1][:], 2 * q + cc, False, cc == 1)
                 nc.scalar.activation(
@@ -241,10 +256,15 @@ def tile_list_carousel_tile_freshness_kernel(
                     ACT.Abs,
                 )
 
+        z_w0 = kt("z_w0", [P, T2], U32)
+        z_s0 = kt("z_s0", [P, T2], U8)
         z_w = {}
-        z_s = {(b, h): kt(f"z_s{b}{h}", [P, 512], U8) for b in range(2) for h in range(2)}
-        for b, h in ((0, 0), (0, 1), (1, 0), (1, 1)):
-            z_w[b, h] = kt(f"z_w{b}{h}", [P, 512], U32)
+        z_s = {}
+        for h in range(2):
+            z_w[0, h] = z_w0[:, 512 * h : 512 * h + 512]
+            z_s[0, h] = z_s0[:, 512 * h : 512 * h + 512]
+            z_w[1, h] = kt(f"z_w1{h}", [P, 512], U32)
+            z_s[1, h] = kt(f"z_s1{h}", [P, 512], U8)
 
         def back(q, zi):
             bank = psum.tile([P, 2, 2, P], F32, name="d2", tag="x", bufs=4)
@@ -259,79 +279,83 @@ def tile_list_carousel_tile_freshness_kernel(
                 bank[:].rearrange("p cc u m -> p cc m u"),
             )
 
-        def back_half(h, dst):
-            bank = psum.tile([P, 4, P], F32, name="d3", tag="y", bufs=2)
-            for cc in range(4):
-                nc.tensor.transpose(bank[:, cc, :], zt[0, h][:].bitcast(F32)[:, 128 * cc : 128 * cc + 128], ident[:])
-            for k in (1, 0):
-                nc.scalar.copy(
-                    dst[k][:].bitcast(F32).rearrange("p (mm u x) -> p mm u x", u=2, x=4)[:, :, 0, :],
-                    bank[:, 2 * k : 2 * k + 2, :].rearrange("p cc (mm x) -> p (cc mm) x", x=4),
-                )
+        def back_half(q, dst):
+            bank = psum.tile([P, 2, P], F32, name="d3", tag="x", bufs=4)
+            for cc in range(2):
+                c = 2 * (q % 2) + cc
+                nc.tensor.transpose(bank[:, cc, :], zt[0, q // 2][:].bitcast(F32)[:, 128 * c : 128 * c + 128], ident[:])
+            nc.scalar.copy(
+                dst[:].bitcast(F32).rearrange("p (mm u x) -> p mm u x", u=2, x=4)[:, :, 0, :],
+                bank[:].rearrange("p cc (mm x) -> p (cc mm) x", x=4),
+            )
 
         def quant_z(b, m0, m1, zi):
             h, c0, c1 = m0 // 512, m0 % 512, (m1 - 1) % 512 + 1
             nc.vector.quantize_mx(out=z_w[b, h][:, c0:c1].bitcast(FP8X4), scales=z_s[b, h][:, c0:c1], in_=zi)
 
-        t0 = rt("ta0", S, "r0"), rt("sb0", S, "r1")
-        t12 = rt("ta1", 2 * S, "taB"), rt("sb1", 2 * S, "sbB")
-        t3 = rt("ta3", S, "taA"), rt("sb3", S, "sbA")
-        appeal(0, t0[1][:], "y", 2)
+        acts[0] = rt("ta0", S, "r0"), rt("sb0", S, "r1")
+        for s in range(1, 4):
+            act_tiles(s)
+        appeal(0, acts[0][1][:], "w", 4)
         make_gw(0, rt("gw0", S, "r4")[:])
-        taste(0, t0[0][:])
-        taste(1, t12[0][:, 0:S])
-        taste(2, t12[0][:, S : 2 * S])
-        taste(3, t3[0][:])
-        appeal(1, t12[1][:, 0:S], "x", 4)
-        appeal(2, t12[1][:, S : 2 * S], "x", 4)
-        appeal(3, t3[1][:], "x", 4)
-        combine([0], *t0, rt("ns0", S, "r2"))
+        for s in range(4):
+            taste(s, acts[s][0][:])
+        for s in range(1, 4):
+            appeal(s, acts[s][1][:], "x", 4)
+        combine(0)
         make_gw(1, rt("gw1", S, "r0")[:])
         make_gw(2, rt("gw2", S, "r1")[:])
-        new_page(1, "r3")
+        new_page(1, "wb_raw1")
         scatter(0)
         new_page(2, "r4")
-        combine([1, 2], *t12, kt("ns12", [P, 2 * S], F32))
+        for s in range(1, 4):
+            combine(s)
         scatter(1)
         new_page(3, "r0")
         scatter(2)
-        held = ring.tile([P, 4096], BF16, name="g1", tag="held", align_bytes=64)
+        g1 = ring.tile([P, 4096], BF16, name="g1", tag="held", align_bytes=64)
         for a in range(2):
             for h in range(2):
-                cast_wa(nc.scalar.copy, held[:, 2048 * a : 2048 * a + 2048], wa_raw[a, 1, 0], 256 * h, 256 * h + 256, 0)
-        for a in range(2):
-            quant_wa(a, 1, held[:, 2048 * a : 2048 * a + 2048], 0, 512)
-        gw_late = rt("gw_late", 5 * S, "r2")
-        for s in range(3, 8):
+                cast_wa(nc.scalar.copy, g1[:, 2048 * a : 2048 * a + 2048], wa_raw[a, 1, 0], 256 * h, 256 * h + 256, 0)
+        nc.vector.quantize_mx(out=wa_w1[:].bitcast(FP8X4), scales=wa_s1[:], in_=g1[:])
+        gw_late = rt("gw_late", 4 * S, "wa_raw110")
+        make_gw(3, gw_late[:, 0:S])
+        diff_close(0, 0, diff_open(0, 0, range(4), "x"))
+        for s in range(4, 7):
             make_gw(s, gw_late[:, (s - 3) * S : (s - 2) * S])
-        diff_pair(0, 0, range(4))
-        ns3 = ring.tile([P, S], F32, name="ns3", tag="held", align_bytes=64)
-        combine([3], *t3, ns3)
-        t4 = group([4], "C")
         scatter(3)
-        t56 = group([5, 6], "B")
-        t7 = group([7], "A")
-        combine([4], *t4, kt("ns4", [P, S], F32))
+        for s in (4, 5):
+            act_tiles(s)
+            appeal(s, acts[s][1][:], "x", 4)
+        for s in (4, 5):
+            taste(s, acts[s][0][:])
+        open01 = diff_open(0, 1, range(4), "w")
+        for s in (6, 7):
+            act_tiles(s)
+            taste(s, acts[s][0][:])
+        for s in (6, 7):
+            appeal(s, acts[s][1][:], "x", 4)
+        combine(4)
+        combine(5)
         scatter(4)
-        diff_pair(0, 1, range(4))
-        combine([5, 6], *t56, kt("ns56", [P, 2 * S], F32))
+        diff_close(0, 1, open01)
         scatter(5)
+        combine(6)
+        combine(7)
         zi0 = ring.tile([P, 4096], BF16, name="zi0", tag="held", align_bytes=64)
         for q in range(4):
             back(q, zi0[:, 1024 * q : 1024 * q + 1024])
         scatter(6)
-        for h in range(2):
-            quant_z(0, 512 * h, 512 * h + 512, zi0[:, 2048 * h : 2048 * h + 2048])
+        nc.vector.quantize_mx(out=z_w0[:].bitcast(FP8X4), scales=z_s0[:], in_=zi0[:])
         last = ring.tile([P, 2 * T2], F32, name="last", tag="held", align_bytes=64)
         d = last[:].rearrange("p (e m) -> p e m", e=2)
-        ns7 = d[:, 1, 0:S]
-        combine([7], *t7, ns7)
+        make_gw(7, d[:, 1, 0:S])
         nc.vector.tensor_tensor(d[:, 0, :], pages[2][:], shown_t[1, 1][:, 0, :], ALU.add)
-        diff_pair(1, 0, (2, 3, 0, 1))
+        diff_close(1, 0, diff_open(1, 0, (2, 3, 0, 1), "w"))
         zi1 = [kt(f"zi1{q}", [P, 1024], BF16) for q in range(4)]
         zp = [kt(f"zp{q}", [P, 1024], BF16) for q in range(4)]
-        for h in (1, 0):
-            back_half(h, zp[2 * h : 2 * h + 2])
+        for q in (3, 2, 1, 0):
+            back_half(q, zp[q])
         scatter(7)
 
         def final_pass(dst, n, m0, m1, b, start, stop):
@@ -344,16 +368,18 @@ def tile_list_carousel_tile_freshness_kernel(
 
         acc_a = []
         for q in range(4):
-            acc_a.append(psum.tile([P, 2, 256], F32, name="acca", tag="x", bufs=4))
+            acc_a.append(psum.tile([P, 2, 256], F32, name="acca", tag="w", bufs=4))
             for n in range(2):
                 final_pass(acc_a[q][:, n, :], n, 256 * q, 256 * q + 256, 0, n == 0, False)
         acc_b = []
         for h in range(2):
-            acc_b.append(psum.tile([P, 512], F32, name="accb", tag="y", bufs=2))
+            acc_b.append(psum.tile([P, 512], F32, name="accb", tag="x", bufs=4))
             final_pass(acc_b[h][:], 2, 512 * h, 512 * h + 512, 0, True, False)
         for q in range(4):
             cols = slice(256 * q, 256 * q + 256)
-            nc.vector.tensor_tensor(d[:, 1, cols], pages[3][:, cols], shown_t[1, 1][:, 1, cols], ALU.add)
+            if q % 2 == 0:
+                half = slice(256 * q, 256 * q + 512)
+                nc.vector.tensor_tensor(d[:, 1, half], pages[3][:, half], shown_t[1, 1][:, 1, half], ALU.add)
             nc.scalar.activation(
                 zp[q][:].rearrange("p (mm u x e) -> p mm u x e", u=2, x=4, e=2)[:, :, 1, :, :],
                 d[:, :, cols].rearrange("p e (mm x) -> p mm x e", x=4),

@@ -48,7 +48,8 @@ def tile_list_carousel_tile_freshness_kernel(
             pages[i] = ring.tile([P, T2], F32, name=f"page{i}", tag=tag, align_bytes=64)
             nc.gpsimd.memset(pages[i][:], 0.0)
 
-        new_page(0, "page0")
+        for i in range(4):
+            new_page(i, f"page{i}")
         ident = kt("ident", [P, P], F32)
         make_identity(nc, ident[:])
 
@@ -144,7 +145,7 @@ def tile_list_carousel_tile_freshness_kernel(
             )
 
         def cast_wa(copy, grouped, raw, c0, c1, r0):
-            dst = grouped[:].rearrange("p (t mm mp j) -> p mm j mp t", t=4, mp=2, j=4)[:, c0 // 8 : c1 // 8]
+            dst = grouped.rearrange("p t (mm mp j) -> p mm j mp t", mp=2, j=4)[:, c0 // 8 : c1 // 8]
             src = raw[:, :, c0 - r0 : c1 - r0].rearrange("p j (mm mp t) -> p mm j mp t", mp=2, t=4)
             copy(dst, src)
 
@@ -158,8 +159,6 @@ def tile_list_carousel_tile_freshness_kernel(
         for a in range(2):
             wa_w[a, 0] = kt(f"wa_w{a}0", [P, 512], U32)
             wa_s[a, 0] = kt(f"wa_s{a}0", [P, 512], U8)
-            wa_w[a, 1] = wa_w1[:, 512 * a : 512 * a + 512]
-            wa_s[a, 1] = wa_s1[:, 512 * a : 512 * a + 512]
 
         g00 = kt("g00", [P, 2048], BF16)
         g10 = ring.tile([P, 2048], BF16, name="g10", tag="r3", align_bytes=64)
@@ -167,37 +166,47 @@ def tile_list_carousel_tile_freshness_kernel(
         gather_scales(0)
         gather_scales(1)
         permute_wb_words(0)
-        cast_wa(nc.scalar.copy, g00, wa_raw[0, 0, 0], 0, 256, 0)
-        cast_wa(nc.vector.tensor_copy, g00, wa_raw[0, 0, 0], 256, 512, 0)
+        cast_wa(nc.scalar.copy, g00[:].rearrange("p (t x) -> p t x", t=4), wa_raw[0, 0, 0], 0, 256, 0)
+        cast_wa(nc.vector.tensor_copy, g00[:].rearrange("p (t x) -> p t x", t=4), wa_raw[0, 0, 0], 256, 512, 0)
         quant_wa(0, 0, g00, 0, 512)
         permute_wb_scales(0)
         permute_wb_scales(1)
         gather_words(1)
-        cast_wa(nc.vector.tensor_copy, g10, wa_raw[1, 0, 0], 0, 256, 0)
-        cast_wa(nc.scalar.copy, g10, wa_raw[1, 0, 256], 256, 368, 256)
-        cast_wa(nc.vector.tensor_copy, g10, wa_raw[1, 0, 256], 368, 512, 256)
+        cast_wa(nc.vector.tensor_copy, g10[:].rearrange("p (t x) -> p t x", t=4), wa_raw[1, 0, 0], 0, 256, 0)
+        cast_wa(nc.scalar.copy, g10[:].rearrange("p (t x) -> p t x", t=4), wa_raw[1, 0, 256], 256, 368, 256)
+        cast_wa(nc.vector.tensor_copy, g10[:].rearrange("p (t x) -> p t x", t=4), wa_raw[1, 0, 256], 368, 512, 256)
         quant_wa(1, 0, g10, 0, 128)
         quant_wa(1, 0, g10, 128, 256)
         quant_wa(1, 0, g10, 256, 512)
         permute_wb_words(1)
 
         gw = {}
+        ngain = kt("ngain", [P, 2, 4], F32)
+        nc.scalar.activation(ngain[:], gain_t[:], ACT.Copy, scale=-1.0)
 
         def make_gw(s, dst):
             b, i = divmod(s, 4)
             gw[s] = dst
-            nc.scalar.activation(dst, wgs_t[:], ACT.Copy, scale=gain_t[:, b, i : i + 1])
+            nc.scalar.activation(dst, wgs_t[:], ACT.Copy, scale=ngain[:, b, i : i + 1])
 
-        def taste(s, ta):
+        def taste_sum(s):
             b, i = divmod(s, 4)
             cols = slice(128 * i, 128 * i + 128)
             pa = psum.tile([P, S], F32, name="pa", tag="x", bufs=4)
             for a in range(2):
+                if b == 0:
+                    words, scales = wa_w[a, 0][:, cols], wa_s[a, 0][:, cols]
+                else:
+                    c0 = 256 * i + 128 * a
+                    words, scales = wa_w1[:, c0 : c0 + 128], wa_s1[:, c0 : c0 + 128]
                 nc.tensor.matmul_mx(
-                    out=pa[:], lhsT=wa_w[a, b][:, cols].bitcast(FP8X4), lhsT_scale=wa_s[a, b][:, cols],
+                    out=pa[:], lhsT=words.bitcast(FP8X4), lhsT_scale=scales,
                     rhs=v_w[a][:].bitcast(FP8X4), rhs_scale=v_s[a][:], start=(a == 0), stop=(a == 1),
                 )
-            nc.scalar.activation(ta, pa[:], ACT.Tanh)
+            return pa
+
+        def taste(s, ta):
+            nc.scalar.activation(ta, taste_sum(s)[:], ACT.Tanh)
 
         def appeal(s, sb, tag, bufs):
             c0 = 128 * s
@@ -219,13 +228,15 @@ def tile_list_carousel_tile_freshness_kernel(
         def act_tiles(s):
             acts[s] = rt(f"ta{s}", S, f"ta{s % 4}"), rt(f"sb{s}", S, f"sb{s % 4}")
 
-        def combine(s):
-            nsum[s] = rt(f"ns{s}", S, f"ns{s % 4}")[:]
+        def combine(s, eng, tag):
             ta, sb = acts[s]
-            nc.vector.scalar_tensor_tensor(out=nsum[s], in0=ta[:], scalar=-1.0, in1=sb[:], op0=ALU.mult, op1=ALU.subtract)
+            both = rt(f"both{s}", S, tag)
+            eng.tensor_tensor(both[:], ta[:], sb[:], ALU.add)
+            nsum[s] = rt(f"ns{s}", S, f"ns{s % 4}")[:]
+            eng.tensor_tensor(nsum[s], both[:], gw[s], ALU.mult)
 
         def scatter(s):
-            nc.vector.tensor_tensor(pages[s % 4][:].indirect(offs2_t[:]), nsum[s], gw[s], ALU.mult)
+            nc.vector.tensor_copy(pages[s % 4][:].indirect(offs2_t[:]), nsum[s])
 
         zt = {}
 
@@ -298,59 +309,57 @@ def tile_list_carousel_tile_freshness_kernel(
             act_tiles(s)
         appeal(0, acts[0][1][:], "w", 4)
         make_gw(0, rt("gw0", S, "r4")[:])
-        for s in range(4):
-            taste(s, acts[s][0][:])
-        for s in range(1, 4):
-            appeal(s, acts[s][1][:], "x", 4)
-        combine(0)
-        make_gw(1, rt("gw1", S, "r0")[:])
-        make_gw(2, rt("gw2", S, "r1")[:])
-        new_page(1, "wb_raw1")
+        sums = [taste_sum(s) for s in range(4)]
+        nc.scalar.activation(acts[0][0][:], sums[0][:], ACT.Tanh)
+        combine(0, nc.vector, "both")
         scatter(0)
-        new_page(2, "r4")
         for s in range(1, 4):
-            combine(s)
+            nc.scalar.activation(acts[s][0][:], sums[s][:], ACT.Tanh)
+            appeal(s, acts[s][1][:], "x", 4)
+            if s < 3:
+                make_gw(s, rt(f"gw{s}", S, f"r{s - 1}")[:])
+                combine(s, nc.gpsimd, "both")
         scatter(1)
-        new_page(3, "r0")
         scatter(2)
         g1 = ring.tile([P, 4096], BF16, name="g1", tag="held", align_bytes=64)
         for a in range(2):
             for h in range(2):
-                cast_wa(nc.scalar.copy, g1[:, 2048 * a : 2048 * a + 2048], wa_raw[a, 1, 0], 256 * h, 256 * h + 256, 0)
-        nc.vector.quantize_mx(out=wa_w1[:].bitcast(FP8X4), scales=wa_s1[:], in_=g1[:])
+                cast_wa(nc.scalar.copy, g1[:].rearrange("p (t a x) -> p t a x", t=4, a=2)[:, :, a, :], wa_raw[a, 1, 0], 256 * h, 256 * h + 256, 0)
+        for c0, c1 in ((0, 256), (256, 512), (512, 1024)):
+            nc.vector.quantize_mx(out=wa_w1[:, c0:c1].bitcast(FP8X4), scales=wa_s1[:, c0:c1], in_=g1[:, 4 * c0 : 4 * c1])
         gw_late = rt("gw_late", 4 * S, "wa_raw110")
         make_gw(3, gw_late[:, 0:S])
+        combine(3, nc.gpsimd, "both")
         diff_close(0, 0, diff_open(0, 0, range(4), "x"))
-        for s in range(4, 7):
-            make_gw(s, gw_late[:, (s - 3) * S : (s - 2) * S])
         scatter(3)
         for s in (4, 5):
             act_tiles(s)
             appeal(s, acts[s][1][:], "x", 4)
-        for s in (4, 5):
             taste(s, acts[s][0][:])
+            make_gw(s, gw_late[:, (s - 3) * S : (s - 2) * S])
+        make_gw(6, gw_late[:, 3 * S : 4 * S])
         open01 = diff_open(0, 1, range(4), "w")
         for s in (6, 7):
             act_tiles(s)
             taste(s, acts[s][0][:])
         for s in (6, 7):
             appeal(s, acts[s][1][:], "x", 4)
-        combine(4)
-        combine(5)
+        combine(4, nc.gpsimd, "both")
+        combine(5, nc.gpsimd, "both")
         scatter(4)
         diff_close(0, 1, open01)
         scatter(5)
-        combine(6)
-        combine(7)
+        combine(6, nc.gpsimd, "both")
         zi0 = ring.tile([P, 4096], BF16, name="zi0", tag="held", align_bytes=64)
         for q in range(4):
             back(q, zi0[:, 1024 * q : 1024 * q + 1024])
+        make_gw(7, rt("gw7", S, "zt11")[:])
+        combine(7, nc.gpsimd, "both")
         scatter(6)
         nc.vector.quantize_mx(out=z_w0[:].bitcast(FP8X4), scales=z_s0[:], in_=zi0[:])
-        last = ring.tile([P, 2 * T2], F32, name="last", tag="held", align_bytes=64)
+        last = rt("last", 2 * T2, "both")
         d = last[:].rearrange("p (e m) -> p e m", e=2)
-        make_gw(7, d[:, 1, 0:S])
-        nc.vector.tensor_tensor(d[:, 0, :], pages[2][:], shown_t[1, 1][:, 0, :], ALU.add)
+        nc.gpsimd.tensor_tensor(d[:, 0, :], pages[2][:], shown_t[1, 1][:, 0, :], ALU.add)
         diff_close(1, 0, diff_open(1, 0, (2, 3, 0, 1), "w"))
         zi1 = [kt(f"zi1{q}", [P, 1024], BF16) for q in range(4)]
         zp = [kt(f"zp{q}", [P, 1024], BF16) for q in range(4)]
@@ -368,12 +377,12 @@ def tile_list_carousel_tile_freshness_kernel(
 
         acc_a = []
         for q in range(4):
-            acc_a.append(psum.tile([P, 2, 256], F32, name="acca", tag="w", bufs=4))
+            acc_a.append(psum.tile([P, 2, 256], F32, name="acca", tag="x", bufs=4))
             for n in range(2):
                 final_pass(acc_a[q][:, n, :], n, 256 * q, 256 * q + 256, 0, n == 0, False)
         acc_b = []
         for h in range(2):
-            acc_b.append(psum.tile([P, 512], F32, name="accb", tag="x", bufs=4))
+            acc_b.append(psum.tile([P, 512], F32, name="accb", tag="w", bufs=4))
             final_pass(acc_b[h][:], 2, 512 * h, 512 * h + 512, 0, True, False)
         for q in range(4):
             cols = slice(256 * q, 256 * q + 256)

from contextlib import ExitStack

import concourse.mybir as mybir
from concourse.masks import make_identity

K, T, S, H, T2, N = 1024, 2048, 512, 1024, 1024, 384
FLOPS = 2 * (2 * K * H * S + H * N * T2)

F32 = mybir.dt.float32
BF16 = mybir.dt.bfloat16
I32 = mybir.dt.int32
U32 = mybir.dt.uint32
U16 = mybir.dt.uint16
U8 = mybir.dt.uint8
FP8X4 = mybir.dt.float8_e4m3fn_x4
FP4X4 = mybir.dt.float4_e2m1fn_x4
ALU = mybir.AluOpType
ACT = mybir.ActivationFunctionType
P = 128


def tile_list_carousel_tile_freshness_kernel(
    tc, tab_words, tab_scales, offs, wa, wb_words, wb_scales, gain, offs2, wgs, shown, wf_words, wf_scales, out
):
    nc = tc.nc
    with ExitStack() as ctx:
        keep = ctx.enter_context(tc.tile_pool(name="keep", bufs=1))
        ring = ctx.enter_context(tc.tile_pool(name="ring", bufs=1))
        psum = ctx.enter_context(tc.psum_pool(name="psum", bufs=1))

        def kt(name, shape, dt):
            return keep.tile(shape, dt, name=name, align_bytes=64)

        offs_t = keep.tile([P, S // 16], U16, name="offs_t")
        offs2_t = keep.tile([P, S // 16], U16, name="offs2_t")
        tab_sc = kt("tab_sc", [P, 2, T], U8)
        wb_sc_raw = kt("wb_sc_raw", [P, 2, H], U8)
        wf_sc = kt("wf_sc", [P, N], U8)
        warm = kt("warm", [P, 8], F32)
        nc.gpsimd.memset(tab_sc[:].rearrange("p a t -> p (a t)").bitcast(I32), 0)
        nc.vector.memset(wb_sc_raw[:].rearrange("p a t -> p (a t)").bitcast(I32), 0)
        nc.vector.memset(warm[:], 0.0)
        nc.scalar.activation(warm[:, 4:5], warm[:, 0:1], ACT.Sigmoid)
        nc.vector.memset(wf_sc[:].bitcast(I32), 0)
        pages = {}

        def new_page(i, tag):
            pages[i] = ring.tile([P, T2], F32, name=f"page{i}", tag=tag, align_bytes=64)
            nc.gpsimd.memset(pages[i][:], 0.0)

        for i in range(4):
            new_page(i, f"page{i}")
        ident = kt("ident", [P, P], F32)
        make_identity(nc, ident[:])

        tabw = [kt(f"tabw{a}", [P, T], I32) for a in range(2)]
        wb_raw = [
            ring.tile([P, 2, H // 4], I32, name=f"wb_raw{b}", tag=f"wb_raw{b}", align_bytes=64) for b in range(2)
        ]
        wa_raw = {}

        def load_wa(a, b, c0, c1):
            t = ring.tile([P, 4, c1 - c0], F32, name=f"wa_raw{a}{b}{c0}", tag=f"wa_raw{a}{b}{c0}", align_bytes=64)
            nc.sync.dma_start(
                out=t[:],
                in_=wa[512 * a : 512 * a + 512, 512 * b + c0 : 512 * b + c1].rearrange("(p j) c -> p j c", j=4),
            )
            wa_raw[a, b, c0] = t

        def load_wb(b):
            nc.sync.dma_start(
                out=wb_raw[b][:], in_=wb_words[:, :, H * b : H * b + H].rearrange("a p c -> p a c").bitcast(I32)
            )

        wgs_t = kt("wgs_t", [P, S], F32)
        gain_t = kt("gain_t", [P, 2, 4], F32)
        nc.sync.dma_start(offs_t[:], offs)
        nc.sync.dma_start(out=tabw[0][:], in_=tab_words[0].rearrange("p t i -> p (t i)").bitcast(I32))
        nc.sync.dma_start(offs2_t[:], offs2)
        for q in range(4):
            nc.sync.dma_start(
                out=tab_sc[q:P:32, :, :].bitcast(I32),
                in_=tab_scales[:, q:16:4, :].rearrange("a r t -> r a t").bitcast(I32),
            )
        load_wb(0)
        load_wa(0, 0, 0, 512)
        for q in range(4):
            nc.sync.dma_start(
                out=wb_sc_raw[q:P:32, :, :].bitcast(I32),
                in_=wb_scales[:, q:16:4, :].rearrange("a r t -> r a t").bitcast(I32),
            )
        nc.sync.dma_start(out=tabw[1][:], in_=tab_words[1].rearrange("p t i -> p (t i)").bitcast(I32))
        load_wa(1, 0, 0, 256)
        load_wa(1, 0, 256, 512)
        nc.sync.dma_start(out=wgs_t[:], in_=wgs)
        nc.sync.dma_start(out=gain_t[:], in_=gain.rearrange("(b p i) -> p b i", b=2, i=4))
        load_wb(1)
        shown_t = {}

        def load_shown(b, u):
            shown_t[b, u] = kt(f"shown{b}{u}", [P, 2, T2], F32)
            nc.sync.dma_start(
                out=shown_t[b, u][:],
                in_=shown[512 * b : 512 * b + 512, :].rearrange("(p i) m -> p i m", i=4)[:, 2 * u : 2 * u + 2, :],
            )

        load_shown(0, 0)
        load_wa(0, 1, 0, 512)
        load_wa(1, 1, 0, 512)
        wf_w = [kt(f"wf_w{b}", [P, N], I32) for b in range(2)]
        for b in range(2):
            nc.sync.dma_start(out=wf_w[b][:], in_=wf_words[b].rearrange("p c i -> p (c i)").bitcast(I32))
        load_shown(1, 0)
        load_shown(1, 1)
        load_shown(0, 1)
        for q in range(4):
            nc.sync.dma_start(
                out=wf_sc[32 * q : 32 * q + 8, :].bitcast(I32),
                in_=wf_scales[:, 4 * q : 4 * q + 4, :].bitcast(I32),
            )

        v_w = [kt(f"v_w{a}", [P, S], U32) for a in range(2)]
        v_s = [kt(f"v_s{a}", [P, S], U8) for a in range(2)]
        wb_w = [kt(f"wb_w{b}", [P, 2, H], U8) for b in range(2)]
        wb_s = [kt(f"wb_s{a}", [P, H], U8) for a in range(2)]
        wa_w = {}
        wa_s = {}

        def gather_words(a):
            nc.vector.tensor_copy(v_w[a][:], tabw[a][:].bitcast(U32).indirect(offs_t[:]))

        def gather_scales(a):
            nc.vector.tensor_copy(v_s[a][:], tab_sc[:, a, :].indirect(offs_t[:]))

        def permute_wb_words(b):
            nc.vector.tensor_copy(
                wb_w[b][:].bitcast(U16).rearrange("p a (t m) -> p a m t", t=4),
                wb_raw[b][:].bitcast(U16).rearrange("p a (m t) -> p a m t", t=4),
            )

        def permute_wb_scales(a):
            nc.vector.tensor_copy(
                wb_s[a][:].rearrange("p (b t m) -> p b m t", b=2, t=4),
                wb_sc_raw[:, a, :].rearrange("p (b m t) -> p b m t", b=2, t=4),
            )

        def cast_wa(copy, grouped, raw, c0, c1, r0):
            dst = grouped.rearrange("p t (mm mp j) -> p mm j mp t", mp=2, j=4)[:, c0 // 8 : c1 // 8]
            src = raw[:, :, c0 - r0 : c1 - r0].rearrange("p j (mm mp t) -> p mm j mp t", mp=2, t=4)
            copy(dst, src)

        def quant_wa(a, b, grouped, c0, c1):
            nc.vector.quantize_mx(
                out=wa_w[a, b][:, c0:c1].bitcast(FP8X4), scales=wa_s[a, b][:, c0:c1], in_=grouped[:, 4 * c0 : 4 * c1]
            )

        wa_w1 = kt("wa_w1", [P, 1024], U32)
        wa_s1 = kt("wa_s1", [P, 1024], U8)
        for a in range(2):
            wa_w[a, 0] = kt(f"wa_w{a}0", [P, 512], U32)
            wa_s[a, 0] = kt(f"wa_s{a}0", [P, 512], U8)

        g00 = kt("g00", [P, 2048], BF16)
        g10 = ring.tile([P, 2048], BF16, name="g10", tag="r3", align_bytes=64)
        gather_words(0)
        gather_scales(0)
        gather_scales(1)
        permute_wb_words(0)
        cast_wa(nc.scalar.copy, g00[:].rearrange("p (t x) -> p t x", t=4), wa_raw[0, 0, 0], 0, 256, 0)
        cast_wa(nc.vector.tensor_copy, g00[:].rearrange("p (t x) -> p t x", t=4), wa_raw[0, 0, 0], 256, 512, 0)
        quant_wa(0, 0, g00, 0, 512)
        permute_wb_scales(0)
        permute_wb_scales(1)
        gather_words(1)
        cast_wa(nc.vector.tensor_copy, g10[:].rearrange("p (t x) -> p t x", t=4), wa_raw[1, 0, 0], 0, 256, 0)
        cast_wa(nc.scalar.copy, g10[:].rearrange("p (t x) -> p t x", t=4), wa_raw[1, 0, 256], 256, 368, 256)
        cast_wa(nc.vector.tensor_copy, g10[:].rearrange("p (t x) -> p t x", t=4), wa_raw[1, 0, 256], 368, 512, 256)
        quant_wa(1, 0, g10, 0, 128)
        quant_wa(1, 0, g10, 128, 256)
        quant_wa(1, 0, g10, 256, 512)
        permute_wb_words(1)

        gw = {}
        ngain = kt("ngain", [P, 2, 4], F32)
        nc.scalar.activation(ngain[:], gain_t[:], ACT.Copy, scale=-1.0)

        def make_gw(s, dst):
            b, i = divmod(s, 4)
            gw[s] = dst
            nc.scalar.activation(dst, wgs_t[:], ACT.Copy, scale=ngain[:, b, i : i + 1])

        def taste_sum(s):
            b, i = divmod(s, 4)
            cols = slice(128 * i, 128 * i + 128)
            pa = psum.tile([P, S], F32, name="pa", tag="x", bufs=4)
            for a in range(2):
                if b == 0:
                    words, scales = wa_w[a, 0][:, cols], wa_s[a, 0][:, cols]
                else:
                    c0 = 256 * i + 128 * a
                    words, scales = wa_w1[:, c0 : c0 + 128], wa_s1[:, c0 : c0 + 128]
                nc.tensor.matmul_mx(
                    out=pa[:], lhsT=words.bitcast(FP8X4), lhsT_scale=scales,
                    rhs=v_w[a][:].bitcast(FP8X4), rhs_scale=v_s[a][:], start=(a == 0), stop=(a == 1),
                )
            return pa

        def taste(s, ta):
            nc.scalar.activation(ta, taste_sum(s)[:], ACT.Tanh)

        def appeal(s, sb, tag, bufs):
            c0 = 128 * s
            pb = psum.tile([P, S], F32, name="pb", tag=tag, bufs=bufs)
            for a in range(2):
                nc.tensor.matmul_mx(
                    out=pb[:], lhsT=wb_w[s // 4][:, a, 256 * (s % 4) : 256 * (s % 4) + 256].bitcast(FP4X4), lhsT_scale=wb_s[a][:, c0 : c0 + 128],
                    rhs=v_w[a][:].bitcast(FP8X4), rhs_scale=v_s[a][:], start=(a == 0), stop=(a == 1),
                )
            nc.scalar.activation(sb, pb[:], ACT.Sigmoid)

        nsum = {}

        def rt(name, cols, tag):
            return ring.tile([P, cols], F32, name=name, tag=tag, align_bytes=64)

        acts = {}

        def act_tiles(s):
            acts[s] = rt(f"ta{s}", S, f"ta{s % 4}"), rt(f"sb{s}", S, f"sb{s % 4}")

        def combine(s, eng, tag):
            ta, sb = acts[s]
            both = rt(f"both{s}", S, tag)
            eng.tensor_tensor(both[:], ta[:], sb[:], ALU.add)
            nsum[s] = rt(f"ns{s}", S, f"ns{s % 4}")[:]
            eng.tensor_tensor(nsum[s], both[:], gw[s], ALU.mult)

        def scatter(s):
            nc.vector.tensor_copy(pages[s % 4][:].indirect(offs2_t[:]), nsum[s])

        zt = {}

        def add_transpose(dst, src, c, start, stop):
            nc.tensor.matmul(dst, lhsT=src[:, 128 * c : 128 * c + 128], rhs=ident[:], is_transpose=True, start=start, stop=stop)

        def diff_open(b, u, order, tag):
            bank = {}
            for q in order:
                bank[q] = psum.tile([P, 2, 2, P], F32, name="d1", tag=tag, bufs=4)
                for cc in range(2):
                    for e in range(2):
                        add_transpose(bank[q][:, cc, e, :], shown_t[b, u][:, e, :], 2 * q + cc, cc + e == 0, False)
            for q in order:
                for cc in range(2):
                    add_transpose(bank[q][:, cc, 0, :], pages[2 * u][:], 2 * q + cc, False, False)
            return bank

        def diff_close(b, u, bank):
            for h in range(2):
                zt[u, h] = ring.tile([P, 1024], BF16, name=f"zt{b}{u}{h}", tag=f"zt{u}{h}", align_bytes=64)
            for q in bank:
                for cc in range(2):
                    add_transpose(bank[q][:, cc, 1, :], pages[2 * u + 1][:], 2 * q + cc, False, cc == 1)
                nc.scalar.activation(
                    zt[u, q // 2][:, 512 * (q % 2) : 512 * (q % 2) + 512].rearrange("m (cc p e) -> m cc p e", cc=2, e=2),
                    bank[q][:].rearrange("m cc e p -> m cc p e"),
                    ACT.Abs,
                )

        z_w0 = kt("z_w0", [P, T2], U32)
        z_s0 = kt("z_s0", [P, T2], U8)
        z_w = {}
        z_s = {}
        for h in range(2):
            z_w[0, h] = z_w0[:, 512 * h : 512 * h + 512]
            z_s[0, h] = z_s0[:, 512 * h : 512 * h + 512]
            z_w[1, h] = kt(f"z_w1{h}", [P, 512], U32)
            z_s[1, h] = kt(f"z_s1{h}", [P, 512], U8)

        def back(q, zi):
            bank = psum.tile([P, 2, 2, P], F32, name="d2", tag="x", bufs=4)
            for u in range(2):
                for cc in range(2):
                    c = 2 * (q % 2) + cc
                    nc.tensor.transpose(
                        bank[:, cc, u, :], zt[u, q // 2][:].bitcast(F32)[:, 128 * c : 128 * c + 128], ident[:]
                    )
            nc.scalar.copy(
                zi.bitcast(F32).rearrange("p (cc m u) -> p cc m u", cc=2, u=2),
                bank[:].rearrange("p cc u m -> p cc m u"),
            )

        def back_half(q, dst):
            bank = psum.tile([P, 2, P], F32, name="d3", tag="x", bufs=4)
            for cc in range(2):
                c = 2 * (q % 2) + cc
                nc.tensor.transpose(bank[:, cc, :], zt[0, q // 2][:].bitcast(F32)[:, 128 * c : 128 * c + 128], ident[:])
            nc.scalar.copy(
                dst[:].bitcast(F32).rearrange("p (mm u x) -> p mm u x", u=2, x=4)[:, :, 0, :],
                bank[:].rearrange("p cc (mm x) -> p (cc mm) x", x=4),
            )

        def quant_z(b, m0, m1, zi):
            h, c0, c1 = m0 // 512, m0 % 512, (m1 - 1) % 512 + 1
            nc.vector.quantize_mx(out=z_w[b, h][:, c0:c1].bitcast(FP8X4), scales=z_s[b, h][:, c0:c1], in_=zi)

        acts[0] = rt("ta0", S, "r0"), rt("sb0", S, "r1")
        for s in range(1, 4):
            act_tiles(s)
        appeal(0, acts[0][1][:], "w", 4)
        make_gw(0, rt("gw0", S, "r4")[:])
        sums = [taste_sum(s) for s in range(4)]
        nc.scalar.activation(acts[0][0][:], sums[0][:], ACT.Tanh)
        combine(0, nc.vector, "both")
        scatter(0)
        for s in range(1, 4):
            nc.scalar.activation(acts[s][0][:], sums[s][:], ACT.Tanh)
            appeal(s, acts[s][1][:], "x", 4)
            if s < 3:
                make_gw(s, rt(f"gw{s}", S, f"r{s - 1}")[:])
                combine(s, nc.gpsimd, "both")
        scatter(1)
        scatter(2)
        g1 = ring.tile([P, 4096], BF16, name="g1", tag="held", align_bytes=64)
        for a in range(2):
            for h in range(2):
                cast_wa(nc.scalar.copy, g1[:].rearrange("p (t a x) -> p t a x", t=4, a=2)[:, :, a, :], wa_raw[a, 1, 0], 256 * h, 256 * h + 256, 0)
        for c0, c1 in ((0, 256), (256, 512), (512, 1024)):
            nc.vector.quantize_mx(out=wa_w1[:, c0:c1].bitcast(FP8X4), scales=wa_s1[:, c0:c1], in_=g1[:, 4 * c0 : 4 * c1])
        gw_late = rt("gw_late", 4 * S, "wa_raw110")
        make_gw(3, gw_late[:, 0:S])
        combine(3, nc.gpsimd, "both")
        diff_close(0, 0, diff_open(0, 0, range(4), "x"))
        scatter(3)
        for s in (4, 5):
            act_tiles(s)
            appeal(s, acts[s][1][:], "x", 4)
            taste(s, acts[s][0][:])
            make_gw(s, gw_late[:, (s - 3) * S : (s - 2) * S])
        make_gw(6, gw_late[:, 3 * S : 4 * S])
        open01 = diff_open(0, 1, range(4), "w")
        for s in (6, 7):
            act_tiles(s)
            taste(s, acts[s][0][:])
        for s in (6, 7):
            appeal(s, acts[s][1][:], "x", 4)
        combine(4, nc.gpsimd, "both")
        combine(5, nc.gpsimd, "both")
        scatter(4)
        diff_close(0, 1, open01)
        scatter(5)
        combine(6, nc.gpsimd, "both")
        zi0 = ring.tile([P, 4096], BF16, name="zi0", tag="held", align_bytes=64)
        for q in range(4):
            back(q, zi0[:, 1024 * q : 1024 * q + 1024])
        make_gw(7, rt("gw7", S, "zt11")[:])
        combine(7, nc.gpsimd, "both")
        scatter(6)
        nc.vector.quantize_mx(out=z_w0[:].bitcast(FP8X4), scales=z_s0[:], in_=zi0[:])
        last = rt("last", 2 * T2, "both")
        d = last[:].rearrange("p (e m) -> p e m", e=2)
        nc.gpsimd.tensor_tensor(d[:, 0, :], pages[2][:], shown_t[1, 1][:, 0, :], ALU.add)
        diff_close(1, 0, diff_open(1, 0, (2, 3, 0, 1), "w"))
        zi1 = [kt(f"zi1{q}", [P, 1024], BF16) for q in range(4)]
        zp = [kt(f"zp{q}", [P, 1024], BF16) for q in range(4)]
        for q in (3, 2, 1, 0):
            back_half(q, zp[q])
        scatter(7)

        def final_pass(dst, n, m0, m1, b, start, stop):
            nc.tensor.matmul_mx(
                out=dst, lhsT=wf_w[b][:, 128 * n : 128 * n + 128].bitcast(FP8X4),
                lhsT_scale=wf_sc[4 * b :, 128 * n : 128 * n + 128],
                rhs=z_w[b, m0 // 512][:, m0 % 512 : (m1 - 1) % 512 + 1].bitcast(FP8X4),
                rhs_scale=z_s[b, m0 // 512][:, m0 % 512 : (m1 - 1) % 512 + 1], start=start, stop=stop,
            )

        acc_a = []
        for q in range(4):
            acc_a.append(psum.tile([P, 2, 256], F32, name="acca", tag="x", bufs=4))
            for n in range(2):
                final_pass(acc_a[q][:, n, :], n, 256 * q, 256 * q + 256, 0, n == 0, False)
        acc_b = []
        for h in range(2):
            acc_b.append(psum.tile([P, 512], F32, name="accb", tag="w", bufs=4))
            final_pass(acc_b[h][:], 2, 512 * h, 512 * h + 512, 0, True, False)
        for q in range(4):
            cols = slice(256 * q, 256 * q + 256)
            if q % 2 == 0:
                half = slice(256 * q, 256 * q + 512)
                nc.vector.tensor_tensor(d[:, 1, half], pages[3][:, half], shown_t[1, 1][:, 1, half], ALU.add)
            nc.scalar.activation(
                zp[q][:].rearrange("p (mm u x e) -> p mm u x e", u=2, x=4, e=2)[:, :, 1, :, :],
                d[:, :, cols].rearrange("p e (mm x) -> p mm x e", x=4),
                ACT.Abs,
            )

        def store_a(q, copy):
            res = ring.tile([P, 2, 256], F32, name=f"resa{q}", tag=f"zt{q // 2}{q % 2}", align_bytes=64)
            copy(res[:], acc_a[q][:])
            nc.sync.dma_start(out=out[0:256, 256 * q : 256 * q + 256].rearrange("(n p) m -> p n m", n=2), in_=res[:])

        def store_b(h, copy):
            res = kt(f"resb{h}", [P, 512], F32)
            copy(res[:], acc_b[h][:])
            nc.sync.dma_start(out=out[256:384, 512 * h : 512 * h + 512], in_=res[:])

        for q in range(4):
            nc.vector.tensor_copy(
                zi1[q][:].bitcast(F32).rearrange("p (mm x u) -> p mm x u", x=4, u=2),
                zp[q][:].bitcast(F32).rearrange("p (mm u x) -> p mm x u", x=4, u=2),
            )
            quant_z(1, 256 * q, 256 * q + 256, zi1[q][:])
            h = q // 2
            for n in range(2):
                final_pass(acc_a[q][:, n, :], n, 256 * q, 256 * q + 256, 1, False, n == 1)
            final_pass(acc_b[h][:, 256 * (q % 2) : 256 * (q % 2) + 256], 2, 256 * q, 256 * q + 256, 1, False, q % 2 == 1)
        store_a(0, nc.scalar.copy)
        store_a(1, nc.scalar.copy)
        store_b(0, nc.scalar.copy)
        store_a(2, nc.vector.tensor_copy)
        store_a(3, nc.vector.tensor_copy)
        store_b(1, nc.scalar.copy)
